import numpy as np
import ml_dtypes


def mxq(x, axis, fmt="e4m3"):
    dtype, down = {"e4m3": (ml_dtypes.float8_e4m3fn, 7), "e5m2": (ml_dtypes.float8_e5m2, 14)}[fmt]
    v = np.moveaxis(np.asarray(x, np.float32).astype(ml_dtypes.bfloat16).astype(np.float64), axis, -1)
    blocks = v.reshape(v.shape[:-1] + (-1, 32))
    amax = np.abs(blocks).max(-1, keepdims=True)
    byte = np.maximum(np.where(amax > 0, np.frexp(amax)[1] - 1 + 127, 0) - down, 1)
    scale = np.exp2(byte - 127.0)
    codes = (blocks / scale).astype(np.float32).astype(dtype).astype(np.float64)
    return np.moveaxis((codes * scale).reshape(v.shape), -1, axis)


WIDE = False


def mx_kscale(k):
    if not WIDE:
        return np.ones(k)
    levels = np.array([10, -10, 5, -5, 0])
    if k % 512:
        return np.exp2(np.random.permutation(np.resize(levels, k // 32))).repeat(32)
    a = np.empty((k // 512, 16))
    for p in range(k // 512):
        a[p, :8] = np.random.permutation(np.resize(levels, 8))
        for g in range(8):
            far = levels[np.abs(levels - a[p, g]) >= 10]
            a[p, g + 8] = far[np.random.randint(len(far))]
    return np.exp2(a.ravel()).repeat(32)


def f64(x):
    return np.asarray(x).astype(np.float64)


def striped(idx):
    return np.tile(idx.reshape(-1, 16).T, (8, 1)).astype(np.uint16)


def unstriped(offs):
    return offs[:16].T.reshape(-1).astype(np.int64)


def striped8(idx):
    return np.concatenate([x.reshape(-1, 16).T for x in idx]).astype(np.uint16)


def runs(offs, k):
    lists = np.stack([offs[16 * r : 16 * r + 16].T.reshape(-1) for r in range(8)]).astype(np.int64)
    return lists[np.arange(k) % 512 // 64]


def pack_weight(w):
    k, n = w.shape
    w = f64(np.asarray(w, np.float32).astype(ml_dtypes.bfloat16)).reshape(k // 32, 32, n)
    amax = np.abs(w).max(1)
    byte = np.clip(np.where(amax > 0, np.frexp(amax)[1] - 1 + 127 - 7, 1), 1, 254)
    scaled = (w * np.exp2(127.0 - byte)[:, None, :]).reshape(k, n).astype(np.float32)
    words = np.ascontiguousarray(scaled.reshape(k // 512, 128, 4, n).transpose(0, 1, 3, 2)).astype(ml_dtypes.float8_e4m3fn).view(np.uint8)
    return words, np.ascontiguousarray(byte.astype(np.uint8).reshape(k // 512, 16, n))


def unpack_weight(words, scales):
    g, p, n, _ = words.shape
    vals = np.ascontiguousarray(words).view(ml_dtypes.float8_e4m3fn).astype(np.float64) * np.repeat(np.exp2(scales.astype(np.float64) - 127.0), 8, axis=1)[..., None]
    return vals.transpose(0, 1, 3, 2).reshape(g * 512, n)


K, T, S, V, N, H = 512, 2048, 512, 256, 512, 512


def setup_inputs():
    n = np.random.standard_normal
    s = mx_kscale(K)[:, None]
    u = mx_kscale(H)
    packed_xT = pack_weight(n((K, T)) * s)
    return {
        "x_words": packed_xT[0],
        "x_scales": packed_xT[1],
        "w1": (n((K, H)) / np.sqrt(K) / s * u).astype(np.float32),
        "t1": (0.5 * n((H, V)) * u[:, None]).astype(np.float32),
        "t2": (0.5 * n((H, V)) * u[:, None]).astype(np.float32),
        "t3": (0.5 * n((H, V)) * u[:, None]).astype(np.float32),
        "w2": (n((H, N)) / np.sqrt(H) / u[:, None]).astype(np.float32),
        "offs": striped(np.random.permutation(T)[:S]),
        "p1": striped8(np.stack([np.random.permutation(S)[:V] for _ in range(8)])),
        "p2": striped8(np.stack([np.random.permutation(S)[:V] for _ in range(8)])),
        "p3": striped8(np.stack([np.random.permutation(S)[:V] for _ in range(8)])),
    }


def reference(x_words, x_scales, w1, t1, t2, t3, w2, offs, p1, p2, p3):
    xq = unpack_weight(x_words, x_scales)[:, unstriped(offs)]
    y = mxq(f64(w1), 0, "e4m3").T @ xq
    z = np.maximum(np.maximum(y[np.arange(H)[:, None], runs(p1, H)] + f64(t1), y[np.arange(H)[:, None], runs(p2, H)] + f64(t2)), y[np.arange(H)[:, None], runs(p3, H)] + f64(t3))
    return mxq(f64(w2), 0, "e4m3").T @ mxq(z, 0, "e4m3")

@@ -1,0 +1,150 @@
+from contextlib import ExitStack
+
+import concourse.mybir as mybir
+
+K, T, S, V, N, H = 512, 2048, 512, 256, 512, 512
+FLOPS = 2 * K * H * S + 2 * H * N * V
+
+F32 = mybir.dt.float32
+BF16 = mybir.dt.bfloat16
+I32 = mybir.dt.int32
+U32 = mybir.dt.uint32
+U16 = mybir.dt.uint16
+U8 = mybir.dt.uint8
+FP8X4 = mybir.dt.float8_e4m3fn_x4
+ADD = mybir.AluOpType.add
+MAX = mybir.AluOpType.max
+
+P = 128
+PACK = 4
+LIST_ROWS = 16
+W1_CUTS = (0, 256, 384, 512)
+W1_LAST_SPLIT = 448
+HALF_N = N // 2
+HALF_S = S // 2
+HALF_V = V // 2
+
+
+def interleave(engine_copy, dst, src):
+    engine_copy(dst.rearrange("p (c i) j -> p c j i", i=4), src.rearrange("p j (c i) -> p c j i", i=4))
+
+
+def tile_picked_tropic_none_p_kernel(
+    tc, x_words, x_scales, w1, t1, t2, t3, w2, offs, p1, p2, p3, out
+):
+    nc = tc.nc
+    with ExitStack() as ctx:
+        keep = ctx.enter_context(tc.tile_pool(name="keep", bufs=1))
+        y_psum = ctx.enter_context(tc.psum_pool(name="y_psum", bufs=5))
+        o_psum = ctx.enter_context(tc.psum_pool(name="o_psum", bufs=1))
+
+        words = keep.tile([P, T], I32, name="words")
+        planes = keep.tile([P, T], U8, name="planes")
+        offs_t = keep.tile([P, S // LIST_ROWS], U16, name="offs_t")
+        lists = [keep.tile([P, V // LIST_ROWS], U16, name=f"list{l}") for l in range(3)]
+        steps = [keep.tile([P, PACK, V], F32, name=f"step{l}") for l in range(3)]
+        w1_raw = [keep.tile([P, PACK, W1_CUTS[c + 1] - W1_CUTS[c]], F32, name=f"w1_raw{c}") for c in range(3)]
+        w2_raw = [keep.tile([P, PACK, HALF_N], F32, name=f"w2_raw{h}") for h in range(2)]
+
+        nc.vector.memset(planes[:].bitcast(I32), 0)
+        nc.sync.dma_start(words[:], x_words[0].rearrange("p n r -> p (n r)").bitcast(I32))
+        nc.sync.dma_start(offs_t[:], offs)
+        for q in range(4):
+            nc.sync.dma_start(planes[32 * q : 32 * q + 4, :].bitcast(I32), x_scales[0, 4 * q : 4 * q + 4, :].bitcast(I32))
+        w1_rows = w1.rearrange("(p j) c -> p j c", j=PACK)
+        for c in range(3):
+            nc.sync.dma_start(w1_raw[c][:], w1_rows[:, :, W1_CUTS[c] : W1_CUTS[c + 1]])
+        w2_rows = w2.rearrange("(p j) c -> p j c", j=PACK)
+
+        def load_step(l, t, p):
+            nc.sync.dma_start(steps[l][:], t.rearrange("(p j) v -> p j v", j=PACK))
+            nc.sync.dma_start(lists[l][:], p)
+
+        load_step(0, t1, p1)
+        nc.sync.dma_start(w2_raw[0][:], w2_rows[:, :, :HALF_N])
+        load_step(1, t2, p2)
+        nc.sync.dma_start(w2_raw[1][:], w2_rows[:, :, HALF_N:])
+        load_step(2, t3, p3)
+
+        x_codes = keep.tile([P, S], U32, name="x_codes", align_bytes=64)
+        x_planes = keep.tile([P, S], U8, name="x_planes", align_bytes=64)
+        for h in range(2):
+            picked = slice(h * HALF_S, (h + 1) * HALF_S)
+            part = offs_t[:, h * HALF_S // LIST_ROWS : (h + 1) * HALF_S // LIST_ROWS]
+            nc.vector.tensor_copy(x_codes[:, picked], words[:].bitcast(U32).indirect(part))
+            nc.vector.tensor_copy(x_planes[:, picked], planes[:].indirect(part))
+
+        w1_bf = keep.tile([P, PACK, P, PACK], BF16, name="w1_bf", align_bytes=64)
+
+        def deal(engine_copy, raw, c0, c1, base):
+            engine_copy(
+                w1_bf[:, :, c0 // PACK : c1 // PACK, :].rearrange("p t m j -> p m j t"),
+                raw[:, :, c0 - base : c1 - base].rearrange("p j (m t) -> p m j t", t=PACK),
+            )
+
+        deal(nc.scalar.copy, w1_raw[0], W1_CUTS[0], W1_CUTS[1], W1_CUTS[0])
+        deal(nc.vector.tensor_copy, w1_raw[1], W1_CUTS[1], W1_CUTS[2], W1_CUTS[1])
+        deal(nc.vector.tensor_copy, w1_raw[2], W1_CUTS[2], W1_LAST_SPLIT, W1_CUTS[2])
+        deal(nc.scalar.copy, w1_raw[2], W1_LAST_SPLIT, H, W1_CUTS[2])
+        w1_codes = keep.tile([P, H], U32, name="w1_codes", align_bytes=64)
+        w1_planes = keep.tile([P, H], U8, name="w1_planes", align_bytes=64)
+        for t in range(PACK):
+            cols = slice(t * P, (t + 1) * P)
+            nc.vector.quantize_mx(w1_codes[:, cols].bitcast(FP8X4), w1_planes[:, cols], w1_bf[:, t].rearrange("p m j -> p (m j)"))
+
+        y = [keep.tile([P, S], F32, name=f"y{t}") for t in range(PACK)]
+        for t in range(PACK):
+            cols = slice(t * P, (t + 1) * P)
+            for h in range(2):
+                picked = slice(h * HALF_S, (h + 1) * HALF_S)
+                acc = y_psum.tile([P, HALF_S], F32, name="acc")
+                nc.tensor.matmul_mx(
+                    acc[:], w1_codes[:, cols].bitcast(FP8X4), w1_planes[:, cols],
+                    x_codes[:, picked].bitcast(FP8X4), x_planes[:, picked], start=True, stop=True,
+                )
+                nc.scalar.copy(y[t][:, picked], acc[:])
+
+        w2_bf = keep.tile([P, N, PACK], BF16, name="w2_bf", align_bytes=64)
+        w2_codes = keep.tile([P, N], U32, name="w2_codes", align_bytes=64)
+        w2_planes = keep.tile([P, N], U8, name="w2_planes", align_bytes=64)
+
+        def candidates(l):
+            cand = keep.tile([P, PACK, V], F32, name=f"cand{l}")
+            for t in range(PACK):
+                nc.vector.tensor_tensor(cand[:, t, :], y[t][:].indirect(lists[l][:]), steps[l][:, t, :], ADD)
+            return cand
+
+        cand_bf = [keep.tile([P, V, PACK], BF16, name=f"cand_bf{l}") for l in range(3)]
+        halves = [slice(h * HALF_V, (h + 1) * HALF_V) for h in range(2)]
+        interleave(nc.scalar.copy, w2_bf[:, :HALF_N, :], w2_raw[0][:])
+        interleave(nc.scalar.copy, cand_bf[0][:], candidates(0)[:])
+        interleave(nc.scalar.copy, w2_bf[:, HALF_N:, :], w2_raw[1][:])
+        interleave(nc.scalar.copy, cand_bf[1][:], candidates(1)[:])
+        last = candidates(2)
+        for states in halves:
+            interleave(nc.scalar.copy, cand_bf[2][:, states, :], last[:, :, states])
+        nc.vector.quantize_mx(w2_codes[:].bitcast(FP8X4), w2_planes[:], w2_bf[:].rearrange("p c j -> p (c j)"))
+        best12 = keep.tile([P, V, PACK], BF16, name="best12")
+        z = keep.tile([P, V, PACK], BF16, name="z", align_bytes=64)
+        for states in halves:
+            nc.vector.tensor_tensor(best12[:, states, :], cand_bf[0][:, states, :], cand_bf[1][:, states, :], MAX)
+        for states in halves:
+            nc.vector.tensor_tensor(z[:, states, :], best12[:, states, :], cand_bf[2][:, states, :], MAX)
+
+        out_rows = out.rearrange("(t p) v -> p t v", p=P)
+        for h, states in enumerate(halves):
+            z_codes = keep.tile([P, HALF_V], U32, name=f"z_codes{h}", align_bytes=64)
+            z_planes = keep.tile([P, HALF_V], U8, name=f"z_planes{h}", align_bytes=64)
+            nc.vector.quantize_mx(z_codes[:].bitcast(FP8X4), z_planes[:], z[:, states, :].rearrange("p v j -> p (v j)"))
+            groups = [(0, 4, nc.scalar.copy, nc.sync)] if h == 0 else [(0, 2, nc.vector.tensor_copy, nc.sync), (2, 4, nc.scalar.copy, nc.scalar)]
+            for ta, tb, engine_copy, queue in groups:
+                acc2 = o_psum.tile([P, tb - ta, HALF_V], F32, name=f"acc2_{h}_{ta}")
+                for t in range(ta, tb):
+                    cols = slice(t * P, (t + 1) * P)
+                    nc.tensor.matmul_mx(
+                        acc2[:, t - ta, :], w2_codes[:, cols].bitcast(FP8X4), w2_planes[:, cols],
+                        z_codes[:].bitcast(FP8X4), z_planes[:], start=True, stop=True,
+                    )
+                res = keep.tile([P, tb - ta, HALF_V], F32, name=f"res_{h}_{ta}")
+                engine_copy(res[:], acc2[:])
+                queue.dma_start(out_rows[:, ta:tb, states], res[:])

@@ -18,8 +18,7 @@ MAX = mybir.AluOpType.max
 P = 128
 PACK = 4
 LIST_ROWS = 16
-W1_CUTS = (0, 256, 384, 512)
-W1_LAST_SPLIT = 448
+W1_VECTOR = 336
 HALF_N = N // 2
 HALF_S = S // 2
 HALF_V = V // 2
@@ -35,7 +34,7 @@ def tile_picked_tropic_none_p_kernel(
     nc = tc.nc
     with ExitStack() as ctx:
         keep = ctx.enter_context(tc.tile_pool(name="keep", bufs=1))
-        y_psum = ctx.enter_context(tc.psum_pool(name="y_psum", bufs=5))
+        y_psum = ctx.enter_context(tc.psum_pool(name="y_psum", bufs=4))
         o_psum = ctx.enter_context(tc.psum_pool(name="o_psum", bufs=1))
 
         words = keep.tile([P, T], I32, name="words")
@@ -43,17 +42,15 @@ def tile_picked_tropic_none_p_kernel(
         offs_t = keep.tile([P, S // LIST_ROWS], U16, name="offs_t")
         lists = [keep.tile([P, V // LIST_ROWS], U16, name=f"list{l}") for l in range(3)]
         steps = [keep.tile([P, PACK, V], F32, name=f"step{l}") for l in range(3)]
-        w1_raw = [keep.tile([P, PACK, W1_CUTS[c + 1] - W1_CUTS[c]], F32, name=f"w1_raw{c}") for c in range(3)]
+        w1_raw = keep.tile([P, PACK, H], F32, name="w1_raw")
         w2_raw = [keep.tile([P, PACK, HALF_N], F32, name=f"w2_raw{h}") for h in range(2)]
 
         nc.vector.memset(planes[:].bitcast(I32), 0)
-        nc.sync.dma_start(words[:], x_words[0].rearrange("p n r -> p (n r)").bitcast(I32))
-        nc.sync.dma_start(offs_t[:], offs)
         for q in range(4):
-            nc.sync.dma_start(planes[32 * q : 32 * q + 4, :].bitcast(I32), x_scales[0, 4 * q : 4 * q + 4, :].bitcast(I32))
-        w1_rows = w1.rearrange("(p j) c -> p j c", j=PACK)
-        for c in range(3):
-            nc.sync.dma_start(w1_raw[c][:], w1_rows[:, :, W1_CUTS[c] : W1_CUTS[c + 1]])
+            nc.scalar.dma_start(planes[32 * q : 32 * q + 4, :].bitcast(I32), x_scales[0, 4 * q : 4 * q + 4, :].bitcast(I32))
+        nc.sync.dma_start(offs_t[:], offs)
+        nc.sync.dma_start(w1_raw[:], w1.rearrange("(p j) c -> p j c", j=PACK))
+        nc.sync.dma_start(words[:], x_words[0].rearrange("p n r -> p (n r)").bitcast(I32))
         w2_rows = w2.rearrange("(p j) c -> p j c", j=PACK)
 
         def load_step(l, t, p):
@@ -66,43 +63,38 @@ def tile_picked_tropic_none_p_kernel(
         nc.sync.dma_start(w2_raw[1][:], w2_rows[:, :, HALF_N:])
         load_step(2, t3, p3)
 
+        w1_bf = keep.tile([P, PACK, P, PACK], BF16, name="w1_bf", align_bytes=64)
+
+        def deal(engine_copy, c0, c1):
+            engine_copy(
+                w1_bf[:, :, c0 // PACK : c1 // PACK, :].rearrange("p t m j -> p m j t"),
+                w1_raw[:, :, c0:c1].rearrange("p j (m t) -> p m j t", t=PACK),
+            )
+
+        deal(nc.scalar.copy, W1_VECTOR, H)
+        deal(nc.vector.tensor_copy, 0, W1_VECTOR)
         x_codes = keep.tile([P, S], U32, name="x_codes", align_bytes=64)
         x_planes = keep.tile([P, S], U8, name="x_planes", align_bytes=64)
+        nc.vector.tensor_copy(x_planes[:], planes[:].indirect(offs_t[:]))
+        w1_codes = keep.tile([P, H], U32, name="w1_codes", align_bytes=64)
+        w1_planes = keep.tile([P, H], U8, name="w1_planes", align_bytes=64)
+        nc.vector.quantize_mx(w1_codes[:].bitcast(FP8X4), w1_planes[:], w1_bf[:].rearrange("p t m j -> p (t m j)"))
         for h in range(2):
             picked = slice(h * HALF_S, (h + 1) * HALF_S)
             part = offs_t[:, h * HALF_S // LIST_ROWS : (h + 1) * HALF_S // LIST_ROWS]
             nc.vector.tensor_copy(x_codes[:, picked], words[:].bitcast(U32).indirect(part))
-            nc.vector.tensor_copy(x_planes[:, picked], planes[:].indirect(part))
-
-        w1_bf = keep.tile([P, PACK, P, PACK], BF16, name="w1_bf", align_bytes=64)
-
-        def deal(engine_copy, raw, c0, c1, base):
-            engine_copy(
-                w1_bf[:, :, c0 // PACK : c1 // PACK, :].rearrange("p t m j -> p m j t"),
-                raw[:, :, c0 - base : c1 - base].rearrange("p j (m t) -> p m j t", t=PACK),
-            )
-
-        deal(nc.scalar.copy, w1_raw[0], W1_CUTS[0], W1_CUTS[1], W1_CUTS[0])
-        deal(nc.vector.tensor_copy, w1_raw[1], W1_CUTS[1], W1_CUTS[2], W1_CUTS[1])
-        deal(nc.vector.tensor_copy, w1_raw[2], W1_CUTS[2], W1_LAST_SPLIT, W1_CUTS[2])
-        deal(nc.scalar.copy, w1_raw[2], W1_LAST_SPLIT, H, W1_CUTS[2])
-        w1_codes = keep.tile([P, H], U32, name="w1_codes", align_bytes=64)
-        w1_planes = keep.tile([P, H], U8, name="w1_planes", align_bytes=64)
-        for t in range(PACK):
-            cols = slice(t * P, (t + 1) * P)
-            nc.vector.quantize_mx(w1_codes[:, cols].bitcast(FP8X4), w1_planes[:, cols], w1_bf[:, t].rearrange("p m j -> p (m j)"))
 
         y = [keep.tile([P, S], F32, name=f"y{t}") for t in range(PACK)]
-        for t in range(PACK):
+        for t, h in [(0, 0), (1, 0), (0, 1), (1, 1), (2, 0), (2, 1), (3, 0), (3, 1)]:
             cols = slice(t * P, (t + 1) * P)
-            for h in range(2):
-                picked = slice(h * HALF_S, (h + 1) * HALF_S)
-                acc = y_psum.tile([P, HALF_S], F32, name="acc")
-                nc.tensor.matmul_mx(
-                    acc[:], w1_codes[:, cols].bitcast(FP8X4), w1_planes[:, cols],
-                    x_codes[:, picked].bitcast(FP8X4), x_planes[:, picked], start=True, stop=True,
-                )
-                nc.scalar.copy(y[t][:, picked], acc[:])
+            picked = slice(h * HALF_S, (h + 1) * HALF_S)
+            acc = y_psum.tile([P, HALF_S], F32, name="acc")
+            nc.tensor.matmul_mx(
+                acc[:], w1_codes[:, cols].bitcast(FP8X4), w1_planes[:, cols],
+                x_codes[:, picked].bitcast(FP8X4), x_planes[:, picked], start=True, stop=True,
+            )
+            empty = nc.vector.tensor_copy if (t, h) == (0, 1) else nc.scalar.copy
+            empty(y[t][:, picked], acc[:])
 
         w2_bf = keep.tile([P, N, PACK], BF16, name="w2_bf", align_bytes=64)
         w2_codes = keep.tile([P, N], U32, name="w2_codes", align_bytes=64)
@@ -136,7 +128,7 @@ def tile_picked_tropic_none_p_kernel(
             z_codes = keep.tile([P, HALF_V], U32, name=f"z_codes{h}", align_bytes=64)
             z_planes = keep.tile([P, HALF_V], U8, name=f"z_planes{h}", align_bytes=64)
             nc.vector.quantize_mx(z_codes[:].bitcast(FP8X4), z_planes[:], z[:, states, :].rearrange("p v j -> p (v j)"))
-            groups = [(0, 4, nc.scalar.copy, nc.sync)] if h == 0 else [(0, 2, nc.vector.tensor_copy, nc.sync), (2, 4, nc.scalar.copy, nc.scalar)]
+            groups = [(0, 2, nc.scalar.copy, nc.scalar), (2, 4, nc.vector.tensor_copy, nc.sync)]
             for ta, tb, engine_copy, queue in groups:
                 acc2 = o_psum.tile([P, tb - ta, HALF_V], F32, name=f"acc2_{h}_{ta}")
                 for t in range(ta, tb):

@@ -18,8 +18,7 @@ MAX = mybir.AluOpType.max
 P = 128
 PACK = 4
 LIST_ROWS = 16
-W1_VECTOR = 336
-HALF_N = N // 2
+W1_VECTOR = 128
 HALF_S = S // 2
 HALF_V = V // 2
 
@@ -34,33 +33,30 @@ def tile_picked_tropic_none_p_kernel(
     nc = tc.nc
     with ExitStack() as ctx:
         keep = ctx.enter_context(tc.tile_pool(name="keep", bufs=1))
-        y_psum = ctx.enter_context(tc.psum_pool(name="y_psum", bufs=4))
-        o_psum = ctx.enter_context(tc.psum_pool(name="o_psum", bufs=1))
+        banks = ctx.enter_context(tc.psum_pool(name="banks", bufs=8))
 
         words = keep.tile([P, T], I32, name="words")
         planes = keep.tile([P, T], U8, name="planes")
         offs_t = keep.tile([P, S // LIST_ROWS], U16, name="offs_t")
         lists = [keep.tile([P, V // LIST_ROWS], U16, name=f"list{l}") for l in range(3)]
-        steps = [keep.tile([P, PACK, V], F32, name=f"step{l}") for l in range(3)]
+        steps = [keep.tile([P, PACK, V], F32, name=f"step{l}", tag=f"step{l}", align_bytes=64) for l in range(3)]
         w1_raw = keep.tile([P, PACK, H], F32, name="w1_raw")
-        w2_raw = [keep.tile([P, PACK, HALF_N], F32, name=f"w2_raw{h}") for h in range(2)]
+        w2_raw = keep.tile([P, PACK, N], F32, name="w2_raw")
 
         nc.vector.memset(planes[:].bitcast(I32), 0)
-        for q in range(4):
-            nc.scalar.dma_start(planes[32 * q : 32 * q + 4, :].bitcast(I32), x_scales[0, 4 * q : 4 * q + 4, :].bitcast(I32))
-        nc.sync.dma_start(offs_t[:], offs)
         nc.sync.dma_start(w1_raw[:], w1.rearrange("(p j) c -> p j c", j=PACK))
+        nc.sync.dma_start(offs_t[:], offs)
+        for q in range(4):
+            nc.sync.dma_start(planes[32 * q : 32 * q + 4, :].bitcast(I32), x_scales[0, 4 * q : 4 * q + 4, :].bitcast(I32))
         nc.sync.dma_start(words[:], x_words[0].rearrange("p n r -> p (n r)").bitcast(I32))
-        w2_rows = w2.rearrange("(p j) c -> p j c", j=PACK)
 
         def load_step(l, t, p):
             nc.sync.dma_start(steps[l][:], t.rearrange("(p j) v -> p j v", j=PACK))
             nc.sync.dma_start(lists[l][:], p)
 
         load_step(0, t1, p1)
-        nc.sync.dma_start(w2_raw[0][:], w2_rows[:, :, :HALF_N])
+        nc.sync.dma_start(w2_raw[:], w2.rearrange("(p j) c -> p j c", j=PACK))
         load_step(1, t2, p2)
-        nc.sync.dma_start(w2_raw[1][:], w2_rows[:, :, HALF_N:])
         load_step(2, t3, p3)
 
         w1_bf = keep.tile([P, PACK, P, PACK], BF16, name="w1_bf", align_bytes=64)
@@ -71,24 +67,30 @@ def tile_picked_tropic_none_p_kernel(
                 w1_raw[:, :, c0:c1].rearrange("p j (m t) -> p m j t", t=PACK),
             )
 
-        deal(nc.scalar.copy, W1_VECTOR, H)
-        deal(nc.vector.tensor_copy, 0, W1_VECTOR)
         x_codes = keep.tile([P, S], U32, name="x_codes", align_bytes=64)
         x_planes = keep.tile([P, S], U8, name="x_planes", align_bytes=64)
+        deal(nc.scalar.copy, W1_VECTOR, H)
+        deal(nc.vector.tensor_copy, 0, W1_VECTOR)
         nc.vector.tensor_copy(x_planes[:], planes[:].indirect(offs_t[:]))
-        w1_codes = keep.tile([P, H], U32, name="w1_codes", align_bytes=64)
+        w1_codes = keep.tile([P, H], U32, name="w1_codes", tag="w1_codes", align_bytes=64)
         w1_planes = keep.tile([P, H], U8, name="w1_planes", align_bytes=64)
-        nc.vector.quantize_mx(w1_codes[:].bitcast(FP8X4), w1_planes[:], w1_bf[:].rearrange("p t m j -> p (t m j)"))
+
+        def quantize_w1(t0, t1):
+            cols = slice(t0 * P, t1 * P)
+            nc.vector.quantize_mx(w1_codes[:, cols].bitcast(FP8X4), w1_planes[:, cols], w1_bf[:, t0:t1].rearrange("p t m j -> p (t m j)"))
+
+        quantize_w1(0, 2)
         for h in range(2):
             picked = slice(h * HALF_S, (h + 1) * HALF_S)
             part = offs_t[:, h * HALF_S // LIST_ROWS : (h + 1) * HALF_S // LIST_ROWS]
             nc.vector.tensor_copy(x_codes[:, picked], words[:].bitcast(U32).indirect(part))
+        quantize_w1(2, 4)
 
-        y = [keep.tile([P, S], F32, name=f"y{t}") for t in range(PACK)]
+        y = [keep.tile([P, S], F32, name=f"y{t}", tag=f"y{t}", align_bytes=64) for t in range(PACK)]
         for t, h in [(0, 0), (1, 0), (0, 1), (1, 1), (2, 0), (2, 1), (3, 0), (3, 1)]:
             cols = slice(t * P, (t + 1) * P)
             picked = slice(h * HALF_S, (h + 1) * HALF_S)
-            acc = y_psum.tile([P, HALF_S], F32, name="acc")
+            acc = banks.tile([P, HALF_S], F32, name="acc", tag="bank")
             nc.tensor.matmul_mx(
                 acc[:], w1_codes[:, cols].bitcast(FP8X4), w1_planes[:, cols],
                 x_codes[:, picked].bitcast(FP8X4), x_planes[:, picked], start=True, stop=True,
@@ -96,8 +98,7 @@ def tile_picked_tropic_none_p_kernel(
             empty = nc.vector.tensor_copy if (t, h) == (0, 1) else nc.scalar.copy
             empty(y[t][:, picked], acc[:])
 
-        w2_bf = keep.tile([P, N, PACK], BF16, name="w2_bf", align_bytes=64)
-        w2_codes = keep.tile([P, N], U32, name="w2_codes", align_bytes=64)
+        w2_bf = keep.tile([P, N, PACK], BF16, name="w2_bf", tag="w1_codes", align_bytes=64)
         w2_planes = keep.tile([P, N], U8, name="w2_planes", align_bytes=64)
 
         def candidates(l):
@@ -106,37 +107,50 @@ def tile_picked_tropic_none_p_kernel(
                 nc.vector.tensor_tensor(cand[:, t, :], y[t][:].indirect(lists[l][:]), steps[l][:, t, :], ADD)
             return cand
 
-        cand_bf = [keep.tile([P, V, PACK], BF16, name=f"cand_bf{l}") for l in range(3)]
         halves = [slice(h * HALF_V, (h + 1) * HALF_V) for h in range(2)]
-        interleave(nc.scalar.copy, w2_bf[:, :HALF_N, :], w2_raw[0][:])
-        interleave(nc.scalar.copy, cand_bf[0][:], candidates(0)[:])
-        interleave(nc.scalar.copy, w2_bf[:, HALF_N:, :], w2_raw[1][:])
-        interleave(nc.scalar.copy, cand_bf[1][:], candidates(1)[:])
+
+        def half_tile(name, tag):
+            return keep.tile([P, HALF_V, PACK], BF16, name=name, tag=tag, align_bytes=64)
+
+        def rounded(l, cand):
+            tiles = []
+            for h, states in enumerate(halves):
+                tiles.append(half_tile(f"cand_bf{l}_{h}", f"cand_bf{l}_{h}"))
+                interleave(nc.scalar.copy, tiles[h][:], cand[:, :, states])
+            return tiles
+
+        interleave(nc.scalar.copy, w2_bf[:], w2_raw[:])
+        c1 = rounded(0, candidates(0))
+        c2 = rounded(1, candidates(1))
         last = candidates(2)
-        for states in halves:
-            interleave(nc.scalar.copy, cand_bf[2][:, states, :], last[:, :, states])
+        c3 = rounded(2, last)
+        best = [half_tile("best0", "y2"), half_tile("best1", "step2")]
+        z = [half_tile(f"z{h}", f"z{h}") for h in range(2)]
+        nc.vector.tensor_tensor(best[0][:], c1[0][:], c2[0][:], MAX)
+        w2_codes = keep.tile([P, N], U32, name="w2_codes", tag="y3", align_bytes=64)
         nc.vector.quantize_mx(w2_codes[:].bitcast(FP8X4), w2_planes[:], w2_bf[:].rearrange("p c j -> p (c j)"))
-        best12 = keep.tile([P, V, PACK], BF16, name="best12")
-        z = keep.tile([P, V, PACK], BF16, name="z", align_bytes=64)
-        for states in halves:
-            nc.vector.tensor_tensor(best12[:, states, :], cand_bf[0][:, states, :], cand_bf[1][:, states, :], MAX)
-        for states in halves:
-            nc.vector.tensor_tensor(z[:, states, :], best12[:, states, :], cand_bf[2][:, states, :], MAX)
+        nc.vector.tensor_tensor(best[1][:], c1[1][:], c2[1][:], MAX)
+        for h in range(2):
+            nc.vector.tensor_tensor(z[h][:], best[h][:], c3[h][:], MAX)
 
         out_rows = out.rearrange("(t p) v -> p t v", p=P)
         for h, states in enumerate(halves):
             z_codes = keep.tile([P, HALF_V], U32, name=f"z_codes{h}", align_bytes=64)
             z_planes = keep.tile([P, HALF_V], U8, name=f"z_planes{h}", align_bytes=64)
-            nc.vector.quantize_mx(z_codes[:].bitcast(FP8X4), z_planes[:], z[:, states, :].rearrange("p v j -> p (v j)"))
-            groups = [(0, 2, nc.scalar.copy, nc.scalar), (2, 4, nc.vector.tensor_copy, nc.sync)]
-            for ta, tb, engine_copy, queue in groups:
-                acc2 = o_psum.tile([P, tb - ta, HALF_V], F32, name=f"acc2_{h}_{ta}")
-                for t in range(ta, tb):
-                    cols = slice(t * P, (t + 1) * P)
-                    nc.tensor.matmul_mx(
-                        acc2[:, t - ta, :], w2_codes[:, cols].bitcast(FP8X4), w2_planes[:, cols],
-                        z_codes[:].bitcast(FP8X4), z_planes[:], start=True, stop=True,
-                    )
-                res = keep.tile([P, tb - ta, HALF_V], F32, name=f"res_{h}_{ta}")
-                engine_copy(res[:], acc2[:])
-                queue.dma_start(out_rows[:, ta:tb, states], res[:])
+            nc.vector.quantize_mx(z_codes[:].bitcast(FP8X4), z_planes[:], z[h][:].rearrange("p v j -> p (v j)"))
+            if h == 0:
+                plan = [[(0, 2, nc.scalar.copy)], [(2, 4, nc.scalar.copy)]]
+            else:
+                plan = [[(0, 2, nc.vector.tensor_copy)], [(2, 3, nc.scalar.copy), (3, 4, nc.vector.tensor_copy)]]
+            for pair, groups in enumerate(plan):
+                res = keep.tile([P, 2, HALF_V], F32, name=f"res_{h}_{pair}")
+                for ta, tb, engine_copy in groups:
+                    acc2 = banks.tile([P, tb - ta, HALF_V], F32, name="acc2", tag="bank")
+                    for t in range(ta, tb):
+                        cols = slice(t * P, (t + 1) * P)
+                        nc.tensor.matmul_mx(
+                            acc2[:, t - ta, :], w2_codes[:, cols].bitcast(FP8X4), w2_planes[:, cols],
+                            z_codes[:].bitcast(FP8X4), z_planes[:], start=True, stop=True,
+                        )
+                    engine_copy(res[:, ta - 2 * pair : tb - 2 * pair, :], acc2[:])
+                nc.sync.dma_start(out_rows[:, 2 * pair : 2 * pair + 2, states], res[:])

@@ -35,7 +35,7 @@ def tile_picked_tropic_none_p_kernel(
         keep = ctx.enter_context(tc.tile_pool(name="keep", bufs=1))
         banks = ctx.enter_context(tc.psum_pool(name="banks", bufs=8))
 
-        words = keep.tile([P, T], I32, name="words")
+        words = keep.tile([P, T], I32, name="words", tag="words", align_bytes=64)
         planes = keep.tile([P, T], U8, name="planes")
         offs_t = keep.tile([P, S // LIST_ROWS], U16, name="offs_t")
         lists = [keep.tile([P, V // LIST_ROWS], U16, name=f"list{l}") for l in range(3)]
@@ -72,33 +72,37 @@ def tile_picked_tropic_none_p_kernel(
         deal(nc.scalar.copy, W1_VECTOR, H)
         deal(nc.vector.tensor_copy, 0, W1_VECTOR)
         nc.vector.tensor_copy(x_planes[:], planes[:].indirect(offs_t[:]))
-        w1_codes = keep.tile([P, H], U32, name="w1_codes", tag="w1_codes", align_bytes=64)
+        w1_codes = {}
         w1_planes = keep.tile([P, H], U8, name="w1_planes", align_bytes=64)
 
-        def quantize_w1(t0, t1):
-            cols = slice(t0 * P, t1 * P)
-            nc.vector.quantize_mx(w1_codes[:, cols].bitcast(FP8X4), w1_planes[:, cols], w1_bf[:, t0:t1].rearrange("p t m j -> p (t m j)"))
+        def quantize_w1(pair, tag):
+            cols = slice(pair * 2 * P, (pair + 1) * 2 * P)
+            w1_codes[pair] = keep.tile([P, 2 * P], U32, name=f"w1_codes{pair}", tag=tag, align_bytes=64)
+            nc.vector.quantize_mx(
+                w1_codes[pair][:].bitcast(FP8X4), w1_planes[:, cols], w1_bf[:, 2 * pair : 2 * pair + 2].rearrange("p t m j -> p (t m j)")
+            )
 
-        quantize_w1(0, 2)
+        quantize_w1(0, "w1_codes0")
         for h in range(2):
             picked = slice(h * HALF_S, (h + 1) * HALF_S)
             part = offs_t[:, h * HALF_S // LIST_ROWS : (h + 1) * HALF_S // LIST_ROWS]
             nc.vector.tensor_copy(x_codes[:, picked], words[:].bitcast(U32).indirect(part))
-        quantize_w1(2, 4)
+        quantize_w1(1, "words")
 
         y = [keep.tile([P, S], F32, name=f"y{t}", tag=f"y{t}", align_bytes=64) for t in range(PACK)]
-        for t, h in [(0, 0), (1, 0), (0, 1), (1, 1), (2, 0), (2, 1), (3, 0), (3, 1)]:
+        pieces = [(0, 0, HALF_S), (1, 0, HALF_S), (0, HALF_S, 3 * S // 4), (0, 3 * S // 4, S), (1, HALF_S, S)]
+        pieces = pieces + [(t, h * HALF_S, (h + 1) * HALF_S) for t in (2, 3) for h in range(2)]
+        for t, s0, s1 in pieces:
             cols = slice(t * P, (t + 1) * P)
-            picked = slice(h * HALF_S, (h + 1) * HALF_S)
-            acc = banks.tile([P, HALF_S], F32, name="acc", tag="bank")
+            picked = slice(s0, s1)
+            acc = banks.tile([P, s1 - s0], F32, name="acc", tag="bank")
             nc.tensor.matmul_mx(
-                acc[:], w1_codes[:, cols].bitcast(FP8X4), w1_planes[:, cols],
+                acc[:], w1_codes[t // 2][:, (t % 2) * P : (t % 2 + 1) * P].bitcast(FP8X4), w1_planes[:, cols],
                 x_codes[:, picked].bitcast(FP8X4), x_planes[:, picked], start=True, stop=True,
             )
-            empty = nc.vector.tensor_copy if (t, h) == (0, 1) else nc.scalar.copy
-            empty(y[t][:, picked], acc[:])
+            nc.scalar.copy(y[t][:, picked], acc[:])
 
-        w2_bf = keep.tile([P, N, PACK], BF16, name="w2_bf", tag="w1_codes", align_bytes=64)
+        w2_bf = keep.tile([P, N, PACK], BF16, name="w2_bf", tag="words", align_bytes=64)
         w2_planes = keep.tile([P, N], U8, name="w2_planes", align_bytes=64)
 
         def candidates(l):
@@ -127,17 +131,29 @@ def tile_picked_tropic_none_p_kernel(
         best = [half_tile("best0", "y2"), half_tile("best1", "step2")]
         z = [half_tile(f"z{h}", f"z{h}") for h in range(2)]
         nc.vector.tensor_tensor(best[0][:], c1[0][:], c2[0][:], MAX)
-        w2_codes = keep.tile([P, N], U32, name="w2_codes", tag="y3", align_bytes=64)
-        nc.vector.quantize_mx(w2_codes[:].bitcast(FP8X4), w2_planes[:], w2_bf[:].rearrange("p c j -> p (c j)"))
+        w2_codes = {}
+
+        def quantize_w2(pair, tag):
+            cols = slice(pair * 2 * P, (pair + 1) * 2 * P)
+            w2_codes[pair] = keep.tile([P, 2 * P], U32, name=f"w2_codes{pair}", tag=tag, align_bytes=64)
+            nc.vector.quantize_mx(w2_codes[pair][:].bitcast(FP8X4), w2_planes[:, cols], w2_bf[:, cols, :].rearrange("p c j -> p (c j)"))
+
+        quantize_w2(0, "y3")
         nc.vector.tensor_tensor(best[1][:], c1[1][:], c2[1][:], MAX)
         for h in range(2):
             nc.vector.tensor_tensor(z[h][:], best[h][:], c3[h][:], MAX)
-
-        out_rows = out.rearrange("(t p) v -> p t v", p=P)
-        for h, states in enumerate(halves):
+        z_mx = []
+        for h in range(2):
             z_codes = keep.tile([P, HALF_V], U32, name=f"z_codes{h}", align_bytes=64)
             z_planes = keep.tile([P, HALF_V], U8, name=f"z_planes{h}", align_bytes=64)
             nc.vector.quantize_mx(z_codes[:].bitcast(FP8X4), z_planes[:], z[h][:].rearrange("p v j -> p (v j)"))
+            z_mx.append((z_codes, z_planes))
+            if h == 0:
+                quantize_w2(1, "y2")
+
+        out_rows = out.rearrange("(t p) v -> p t v", p=P)
+        for h, states in enumerate(halves):
+            z_codes, z_planes = z_mx[h]
             if h == 0:
                 plan = [[(0, 2, nc.scalar.copy)], [(2, 4, nc.scalar.copy)]]
             else:
@@ -149,7 +165,7 @@ def tile_picked_tropic_none_p_kernel(
                     for t in range(ta, tb):
                         cols = slice(t * P, (t + 1) * P)
                         nc.tensor.matmul_mx(
-                            acc2[:, t - ta, :], w2_codes[:, cols].bitcast(FP8X4), w2_planes[:, cols],
+                            acc2[:, t - ta, :], w2_codes[pair][:, (t % 2) * P : (t % 2 + 1) * P].bitcast(FP8X4), w2_planes[:, cols],
                             z_codes[:].bitcast(FP8X4), z_planes[:], start=True, stop=True,
                         )
                     engine_copy(res[:, ta - 2 * pair : tb - 2 * pair, :], acc2[:])

@@ -41,7 +41,7 @@ def tile_picked_tropic_none_p_kernel(
         lists = [keep.tile([P, V // LIST_ROWS], U16, name=f"list{l}") for l in range(3)]
         steps = [keep.tile([P, PACK, V], F32, name=f"step{l}", tag=f"step{l}", align_bytes=64) for l in range(3)]
         w1_raw = keep.tile([P, PACK, H], F32, name="w1_raw")
-        w2_raw = keep.tile([P, PACK, N], F32, name="w2_raw")
+        w2_raw = [keep.tile([P, PACK, 2 * P], F32, name=f"w2_raw{pair}") for pair in range(2)]
 
         nc.vector.memset(planes[:].bitcast(I32), 0)
         nc.sync.dma_start(w1_raw[:], w1.rearrange("(p j) c -> p j c", j=PACK))
@@ -50,14 +50,19 @@ def tile_picked_tropic_none_p_kernel(
             nc.sync.dma_start(planes[32 * q : 32 * q + 4, :].bitcast(I32), x_scales[0, 4 * q : 4 * q + 4, :].bitcast(I32))
         nc.sync.dma_start(words[:], x_words[0].rearrange("p n r -> p (n r)").bitcast(I32))
 
-        def load_step(l, t, p):
-            nc.sync.dma_start(steps[l][:], t.rearrange("(p j) v -> p j v", j=PACK))
-            nc.sync.dma_start(lists[l][:], p)
+        w2_rows = w2.rearrange("(p j) c -> p j c", j=PACK)
 
-        load_step(0, t1, p1)
-        nc.sync.dma_start(w2_raw[:], w2.rearrange("(p j) c -> p j c", j=PACK))
-        load_step(1, t2, p2)
-        load_step(2, t3, p3)
+        def load_step(l, t):
+            nc.sync.dma_start(steps[l][:], t.rearrange("(p j) v -> p j v", j=PACK))
+
+        nc.sync.dma_start(lists[0][:], p1)
+        load_step(0, t1)
+        nc.sync.dma_start(lists[1][:], p2)
+        nc.sync.dma_start(lists[2][:], p3)
+        nc.sync.dma_start(w2_raw[0][:], w2_rows[:, :, : 2 * P])
+        load_step(1, t2)
+        nc.sync.dma_start(w2_raw[1][:], w2_rows[:, :, 2 * P :])
+        load_step(2, t3)
 
         w1_bf = keep.tile([P, PACK, P, PACK], BF16, name="w1_bf", align_bytes=64)
 
@@ -123,7 +128,8 @@ def tile_picked_tropic_none_p_kernel(
                 interleave(nc.scalar.copy, tiles[h][:], cand[:, :, states])
             return tiles
 
-        interleave(nc.scalar.copy, w2_bf[:], w2_raw[:])
+        for pair in range(2):
+            interleave(nc.scalar.copy, w2_bf[:, pair * 2 * P : (pair + 1) * 2 * P, :], w2_raw[pair][:])
         c1 = rounded(0, candidates(0))
         c2 = rounded(1, candidates(1))
         last = candidates(2)

@@ -18,7 +18,6 @@ MAX = mybir.AluOpType.max
 P = 128
 PACK = 4
 LIST_ROWS = 16
-W1_VECTOR = 128
 HALF_S = S // 2
 HALF_V = V // 2
 
@@ -39,44 +38,39 @@ def tile_picked_tropic_none_p_kernel(
         planes = keep.tile([P, T], U8, name="planes")
         offs_t = keep.tile([P, S // LIST_ROWS], U16, name="offs_t")
         lists = [keep.tile([P, V // LIST_ROWS], U16, name=f"list{l}") for l in range(3)]
-        steps = [keep.tile([P, PACK, V], F32, name=f"step{l}", tag=f"step{l}", align_bytes=64) for l in range(3)]
         w1_raw = keep.tile([P, PACK, H], F32, name="w1_raw")
-        w2_raw = [keep.tile([P, PACK, 2 * P], F32, name=f"w2_raw{pair}") for pair in range(2)]
+        x_rows = keep.tile([P, S], U8, name="x_rows", align_bytes=64)
+        x_planes = keep.tile([P, S], U8, name="x_planes", align_bytes=64)
+        warm = keep.tile([P, 2], F32, name="warm")
 
-        nc.vector.memset(planes[:].bitcast(I32), 0)
-        nc.sync.dma_start(w1_raw[:], w1.rearrange("(p j) c -> p j c", j=PACK))
+        nc.scalar.dma_start(planes[16:32, :].bitcast(I32), x_scales[0].bitcast(I32))
+        nc.gpsimd.memset(warm[:, 0:1], 0.0)
+        nc.scalar.copy(warm[:, 1:2], warm[:, 0:1])
+        nc.vector.memset(planes[0:16, :].bitcast(I32), 0)
+        nc.vector.memset(planes[32:64, :].bitcast(I32), 0)
+        nc.vector.memset(planes[64:P, :].bitcast(I32), 0)
+        nc.gpsimd.memset(x_planes[:].bitcast(I32), 0)
         nc.sync.dma_start(offs_t[:], offs)
-        for q in range(4):
-            nc.sync.dma_start(planes[32 * q : 32 * q + 4, :].bitcast(I32), x_scales[0, 4 * q : 4 * q + 4, :].bitcast(I32))
-        nc.sync.dma_start(words[:], x_words[0].rearrange("p n r -> p (n r)").bitcast(I32))
-
-        w2_rows = w2.rearrange("(p j) c -> p j c", j=PACK)
-
-        def load_step(l, t):
-            nc.sync.dma_start(steps[l][:], t.rearrange("(p j) v -> p j v", j=PACK))
-
+        nc.sync.dma_start(w1_raw[:], w1.rearrange("(p j) c -> p j c", j=PACK))
         nc.sync.dma_start(lists[0][:], p1)
-        load_step(0, t1)
+        nc.sync.dma_start(words[:], x_words[0].rearrange("p n r -> p (n r)").bitcast(I32))
         nc.sync.dma_start(lists[1][:], p2)
         nc.sync.dma_start(lists[2][:], p3)
-        nc.sync.dma_start(w2_raw[0][:], w2_rows[:, :, : 2 * P])
-        load_step(1, t2)
-        nc.sync.dma_start(w2_raw[1][:], w2_rows[:, :, 2 * P :])
-        load_step(2, t3)
+        nc.vector.tensor_copy(x_rows[:], planes[:].indirect(offs_t[:]))
+        for q in range(4):
+            nc.scalar.dma_start(x_planes[32 * q : 32 * q + 4, :].bitcast(I32), x_rows[16 + 4 * q : 20 + 4 * q, :].bitcast(I32))
 
-        w1_bf = keep.tile([P, PACK, P, PACK], BF16, name="w1_bf", align_bytes=64)
+        w1_bf = [keep.tile([P, 2, P, PACK], BF16, name=f"w1_bf{pair}", tag=tag, align_bytes=64) for pair, tag in enumerate(("w1_bf0", "late"))]
 
-        def deal(engine_copy, c0, c1):
+        def deal(engine_copy, pair):
             engine_copy(
-                w1_bf[:, :, c0 // PACK : c1 // PACK, :].rearrange("p t m j -> p m j t"),
-                w1_raw[:, :, c0:c1].rearrange("p j (m t) -> p m j t", t=PACK),
+                w1_bf[pair][:].rearrange("p t m j -> p m j t"),
+                w1_raw[:].rearrange("p j (m t) -> p m j t", t=PACK)[:, :, :, 2 * pair : 2 * pair + 2],
             )
 
         x_codes = keep.tile([P, S], U32, name="x_codes", align_bytes=64)
-        x_planes = keep.tile([P, S], U8, name="x_planes", align_bytes=64)
-        deal(nc.scalar.copy, W1_VECTOR, H)
-        deal(nc.vector.tensor_copy, 0, W1_VECTOR)
-        nc.vector.tensor_copy(x_planes[:], planes[:].indirect(offs_t[:]))
+        deal(nc.scalar.copy, 0)
+        deal(nc.vector.tensor_copy, 1)
         w1_codes = {}
         w1_planes = keep.tile([P, H], U8, name="w1_planes", align_bytes=64)
 
@@ -84,19 +78,40 @@ def tile_picked_tropic_none_p_kernel(
             cols = slice(pair * 2 * P, (pair + 1) * 2 * P)
             w1_codes[pair] = keep.tile([P, 2 * P], U32, name=f"w1_codes{pair}", tag=tag, align_bytes=64)
             nc.vector.quantize_mx(
-                w1_codes[pair][:].bitcast(FP8X4), w1_planes[:, cols], w1_bf[:, 2 * pair : 2 * pair + 2].rearrange("p t m j -> p (t m j)")
+                w1_codes[pair][:].bitcast(FP8X4), w1_planes[:, cols], w1_bf[pair][:].rearrange("p t m j -> p (t m j)")
             )
 
+        quantize_w1(1, "w1_codes1")
         quantize_w1(0, "w1_codes0")
+
+        late = keep.tile([P, 5 * PACK * V], F32, name="late", tag="late", align_bytes=64)
+        steps = [late[:, l * PACK * V : (l + 1) * PACK * V].rearrange("p (j v) -> p j v", j=PACK) for l in range(3)]
+        w2_cuts = [(0, 2 * P), (2 * P, N)]
+        w2_at = 3 * PACK * V
+        w2_raw = [late[:, w2_at + PACK * c0 : w2_at + PACK * c1].rearrange("p (j c) -> p j c", j=PACK) for c0, c1 in w2_cuts]
+        w2_rows = w2.rearrange("(p j) c -> p j c", j=PACK)
+
+        def load_step(l, t):
+            nc.sync.dma_start(steps[l], t.rearrange("(p j) v -> p j v", j=PACK))
+
+        def load_w2(i):
+            nc.sync.dma_start(w2_raw[i], w2_rows[:, :, w2_cuts[i][0] : w2_cuts[i][1]])
+
+        load_step(0, t1)
+        load_w2(0)
+        load_step(1, t2)
+        load_w2(1)
+        load_step(2, t3)
+
         for h in range(2):
             picked = slice(h * HALF_S, (h + 1) * HALF_S)
             part = offs_t[:, h * HALF_S // LIST_ROWS : (h + 1) * HALF_S // LIST_ROWS]
             nc.vector.tensor_copy(x_codes[:, picked], words[:].bitcast(U32).indirect(part))
-        quantize_w1(1, "words")
+        w2_bf = keep.tile([P, N, PACK], BF16, name="w2_bf", tag="words", align_bytes=64)
 
         y = [keep.tile([P, S], F32, name=f"y{t}", tag=f"y{t}", align_bytes=64) for t in range(PACK)]
         pieces = [(0, 0, HALF_S), (1, 0, HALF_S), (0, HALF_S, 3 * S // 4), (0, 3 * S // 4, S), (1, HALF_S, S)]
-        pieces = pieces + [(t, h * HALF_S, (h + 1) * HALF_S) for t in (2, 3) for h in range(2)]
+        pieces = pieces + [(2, 0, S), (3, 0, S)]
         for t, s0, s1 in pieces:
             cols = slice(t * P, (t + 1) * P)
             picked = slice(s0, s1)
@@ -105,9 +120,9 @@ def tile_picked_tropic_none_p_kernel(
                 acc[:], w1_codes[t // 2][:, (t % 2) * P : (t % 2 + 1) * P].bitcast(FP8X4), w1_planes[:, cols],
                 x_codes[:, picked].bitcast(FP8X4), x_planes[:, picked], start=True, stop=True,
             )
-            nc.scalar.copy(y[t][:, picked], acc[:])
+            engine_copy = nc.vector.tensor_copy if (t, s0) == (1, 0) else nc.scalar.copy
+            engine_copy(y[t][:, picked], acc[:])
 
-        w2_bf = keep.tile([P, N, PACK], BF16, name="w2_bf", tag="words", align_bytes=64)
         w2_planes = keep.tile([P, N], U8, name="w2_planes", align_bytes=64)
 
         def candidates(l):
@@ -128,13 +143,13 @@ def tile_picked_tropic_none_p_kernel(
                 interleave(nc.scalar.copy, tiles[h][:], cand[:, :, states])
             return tiles
 
-        for pair in range(2):
-            interleave(nc.scalar.copy, w2_bf[:, pair * 2 * P : (pair + 1) * 2 * P, :], w2_raw[pair][:])
+        for i in range(2):
+            interleave(nc.scalar.copy, w2_bf[:, w2_cuts[i][0] : w2_cuts[i][1], :], w2_raw[i])
         c1 = rounded(0, candidates(0))
         c2 = rounded(1, candidates(1))
         last = candidates(2)
         c3 = rounded(2, last)
-        best = [half_tile("best0", "y2"), half_tile("best1", "step2")]
+        best = [half_tile("best0", "y2"), half_tile("best1", "late")]
         z = [half_tile(f"z{h}", f"z{h}") for h in range(2)]
         nc.vector.tensor_tensor(best[0][:], c1[0][:], c2[0][:], MAX)
         w2_codes = {}
@@ -161,18 +176,23 @@ def tile_picked_tropic_none_p_kernel(
         for h, states in enumerate(halves):
             z_codes, z_planes = z_mx[h]
             if h == 0:
-                plan = [[(0, 2, nc.scalar.copy)], [(2, 4, nc.scalar.copy)]]
+                plan = [([(0, 2, nc.scalar.copy)], nc.sync), ([(2, 4, nc.scalar.copy)], nc.sync)]
             else:
-                plan = [[(0, 2, nc.vector.tensor_copy)], [(2, 3, nc.scalar.copy), (3, 4, nc.vector.tensor_copy)]]
-            for pair, groups in enumerate(plan):
-                res = keep.tile([P, 2, HALF_V], F32, name=f"res_{h}_{pair}")
+                plan = [
+                    ([(0, 1, nc.vector.tensor_copy), (1, 2, nc.scalar.copy)], nc.sync),
+                    ([(2, 3, nc.vector.tensor_copy)], nc.sync),
+                    ([(3, 4, nc.scalar.copy)], nc.scalar),
+                ]
+            for groups, queue in plan:
+                t0, t1_end = groups[0][0], groups[-1][1]
+                res = keep.tile([P, t1_end - t0, HALF_V], F32, name=f"res_{h}_{t0}")
                 for ta, tb, engine_copy in groups:
                     acc2 = banks.tile([P, tb - ta, HALF_V], F32, name="acc2", tag="bank")
                     for t in range(ta, tb):
                         cols = slice(t * P, (t + 1) * P)
                         nc.tensor.matmul_mx(
-                            acc2[:, t - ta, :], w2_codes[pair][:, (t % 2) * P : (t % 2 + 1) * P].bitcast(FP8X4), w2_planes[:, cols],
+                            acc2[:, t - ta, :], w2_codes[t // 2][:, (t % 2) * P : (t % 2 + 1) * P].bitcast(FP8X4), w2_planes[:, cols],
                             z_codes[:].bitcast(FP8X4), z_planes[:], start=True, stop=True,
                         )
-                    engine_copy(res[:, ta - 2 * pair : tb - 2 * pair, :], acc2[:])
-                nc.sync.dma_start(out_rows[:, 2 * pair : 2 * pair + 2, states], res[:])
+                    engine_copy(res[:, ta - t0 : tb - t0, :], acc2[:])
+                queue.dma_start(out_rows[:, t0:t1_end, states], res[:])

@@ -107,7 +107,7 @@ def tile_picked_tropic_none_p_kernel(
             picked = slice(h * HALF_S, (h + 1) * HALF_S)
             part = offs_t[:, h * HALF_S // LIST_ROWS : (h + 1) * HALF_S // LIST_ROWS]
             nc.vector.tensor_copy(x_codes[:, picked], words[:].bitcast(U32).indirect(part))
-        w2_bf = keep.tile([P, N, PACK], BF16, name="w2_bf", tag="words", align_bytes=64)
+        w2_bf = keep.tile([P, PACK, P, PACK], BF16, name="w2_bf", tag="words", align_bytes=64)
 
         y = [keep.tile([P, S], F32, name=f"y{t}", tag=f"y{t}", align_bytes=64) for t in range(PACK)]
         pieces = [(0, 0, HALF_S), (1, 0, HALF_S), (0, HALF_S, 3 * S // 4), (0, 3 * S // 4, S), (1, HALF_S, S)]
@@ -143,56 +143,73 @@ def tile_picked_tropic_none_p_kernel(
                 interleave(nc.scalar.copy, tiles[h][:], cand[:, :, states])
             return tiles
 
-        for i in range(2):
-            interleave(nc.scalar.copy, w2_bf[:, w2_cuts[i][0] : w2_cuts[i][1], :], w2_raw[i])
+        for pair in range(2):
+            nc.scalar.copy(
+                w2_bf[:, 2 * pair : 2 * pair + 2].rearrange("p t (c i) j -> p c j i t", i=2),
+                w2_raw[pair].rearrange("p j (c i t) -> p c j i t", i=2, t=2),
+            )
         c1 = rounded(0, candidates(0))
         c2 = rounded(1, candidates(1))
         last = candidates(2)
-        c3 = rounded(2, last)
-        best = [half_tile("best0", "y2"), half_tile("best1", "late")]
+        c3 = keep.tile([P, 2, V, 2], BF16, name="c3", align_bytes=64)
+        interleave(nc.scalar.copy, c3[:, 0], last[:, 0:2, :])
+        for states in halves:
+            interleave(nc.scalar.copy, c3[:, 1, states, :], last[:, 2:4, states])
+        best = {}
         z = [half_tile(f"z{h}", f"z{h}") for h in range(2)]
-        nc.vector.tensor_tensor(best[0][:], c1[0][:], c2[0][:], MAX)
+        z_codes = keep.tile([P, V], U32, name="z_codes", align_bytes=64)
+        z_planes = keep.tile([P, V], U8, name="z_planes", align_bytes=64)
         w2_codes = {}
 
-        def quantize_w2(pair, tag):
-            cols = slice(pair * 2 * P, (pair + 1) * 2 * P)
-            w2_codes[pair] = keep.tile([P, 2 * P], U32, name=f"w2_codes{pair}", tag=tag, align_bytes=64)
-            nc.vector.quantize_mx(w2_codes[pair][:].bitcast(FP8X4), w2_planes[:, cols], w2_bf[:, cols, :].rearrange("p c j -> p (c j)"))
+        def best_of_two(h, tag):
+            best[h] = half_tile(f"best{h}", tag)
+            nc.vector.tensor_tensor(best[h][:], c1[h][:], c2[h][:], MAX)
 
-        quantize_w2(0, "y3")
-        nc.vector.tensor_tensor(best[1][:], c1[1][:], c2[1][:], MAX)
-        for h in range(2):
-            nc.vector.tensor_tensor(z[h][:], best[h][:], c3[h][:], MAX)
-        z_mx = []
-        for h in range(2):
-            z_codes = keep.tile([P, HALF_V], U32, name=f"z_codes{h}", align_bytes=64)
-            z_planes = keep.tile([P, HALF_V], U8, name=f"z_planes{h}", align_bytes=64)
-            nc.vector.quantize_mx(z_codes[:].bitcast(FP8X4), z_planes[:], z[h][:].rearrange("p v j -> p (v j)"))
-            z_mx.append((z_codes, z_planes))
-            if h == 0:
-                quantize_w2(1, "y2")
+        def best_of_three(h):
+            nc.vector.tensor_tensor(
+                z[h][:].rearrange("p v (a j) -> p v a j", a=2), best[h][:].rearrange("p v (a j) -> p v a j", a=2),
+                c3[:, :, halves[h], :].rearrange("p a v j -> p v a j"), MAX,
+            )
 
-        out_rows = out.rearrange("(t p) v -> p t v", p=P)
-        for h, states in enumerate(halves):
-            z_codes, z_planes = z_mx[h]
-            if h == 0:
-                plan = [([(0, 2, nc.scalar.copy)], nc.sync), ([(2, 4, nc.scalar.copy)], nc.sync)]
-            else:
-                plan = [
-                    ([(0, 1, nc.vector.tensor_copy), (1, 2, nc.scalar.copy)], nc.sync),
-                    ([(2, 3, nc.vector.tensor_copy)], nc.sync),
-                    ([(3, 4, nc.scalar.copy)], nc.scalar),
-                ]
-            for groups, queue in plan:
-                t0, t1_end = groups[0][0], groups[-1][1]
-                res = keep.tile([P, t1_end - t0, HALF_V], F32, name=f"res_{h}_{t0}")
-                for ta, tb, engine_copy in groups:
-                    acc2 = banks.tile([P, tb - ta, HALF_V], F32, name="acc2", tag="bank")
-                    for t in range(ta, tb):
-                        cols = slice(t * P, (t + 1) * P)
-                        nc.tensor.matmul_mx(
-                            acc2[:, t - ta, :], w2_codes[t // 2][:, (t % 2) * P : (t % 2 + 1) * P].bitcast(FP8X4), w2_planes[:, cols],
-                            z_codes[:].bitcast(FP8X4), z_planes[:], start=True, stop=True,
-                        )
-                    engine_copy(res[:, ta - t0 : tb - t0, :], acc2[:])
-                queue.dma_start(out_rows[:, t0:t1_end, states], res[:])
+        def quantize_z(h):
+            nc.vector.quantize_mx(z_codes[:, halves[h]].bitcast(FP8X4), z_planes[:, halves[h]], z[h][:].rearrange("p v j -> p (v j)"))
+
+        def quantize_w2(ta, tb, tag):
+            codes = keep.tile([P, (tb - ta) * P], U32, name=f"w2_codes{ta}", tag=tag, align_bytes=64)
+            nc.vector.quantize_mx(codes[:].bitcast(FP8X4), w2_planes[:, ta * P : tb * P], w2_bf[:, ta:tb].rearrange("p t m j -> p (t m j)"))
+            for t in range(ta, tb):
+                w2_codes[t] = codes[:, (t - ta) * P : (t - ta + 1) * P]
+
+        best_of_two(0, "y2")
+        quantize_w2(0, 2, "y3")
+        best_of_three(0)
+        best_of_two(1, "late")
+        quantize_z(0)
+        best_of_three(1)
+        quantize_w2(2, 3, "z0")
+        quantize_z(1)
+        quantize_w2(3, 4, "late")
+
+        out_rows = out.rearrange("(a p t) v -> a p t v", a=2, t=2)
+
+        def project(ta, tb, h, dst, engine_copy):
+            acc2 = banks.tile([P, tb - ta, HALF_V], F32, name="acc2", tag="bank")
+            for t in range(ta, tb):
+                nc.tensor.matmul_mx(
+                    acc2[:, t - ta, :], w2_codes[t].bitcast(FP8X4), w2_planes[:, t * P : (t + 1) * P],
+                    z_codes[:, halves[h]].bitcast(FP8X4), z_planes[:, halves[h]], start=True, stop=True,
+                )
+            engine_copy(dst, acc2[:])
+
+        low = [keep.tile([P, 2, HALF_V], F32, name=f"low{h}") for h in range(2)]
+        high = [keep.tile([P, 1, V], F32, name=f"high{t}") for t in range(2)]
+        project(0, 2, 0, low[0][:], nc.scalar.copy)
+        nc.sync.dma_start(out_rows[0][:, :, halves[0]], low[0][:])
+        project(2, 3, 0, high[0][:, :, halves[0]], nc.scalar.copy)
+        project(0, 2, 1, low[1][:], nc.vector.tensor_copy)
+        nc.sync.dma_start(out_rows[0][:, :, halves[1]], low[1][:])
+        project(2, 3, 1, high[0][:, :, halves[1]], nc.scalar.copy)
+        nc.sync.dma_start(out_rows[1][:, 0:1, :], high[0][:])
+        project(3, 4, 0, high[1][:, :, halves[0]], nc.scalar.copy)
+        project(3, 4, 1, high[1][:, :, halves[1]], nc.vector.tensor_copy)
+        nc.sync.dma_start(out_rows[1][:, 1:2, :], high[1][:])

@@ -35,32 +35,31 @@ def tile_picked_tropic_none_p_kernel(
         banks = ctx.enter_context(tc.psum_pool(name="banks", bufs=8))
 
         words = keep.tile([P, T], I32, name="words", tag="words", align_bytes=64)
-        planes = keep.tile([P, T], U8, name="planes")
+        planes = keep.tile([P, T], U8, name="planes", tag="planes", align_bytes=64)
         offs_t = keep.tile([P, S // LIST_ROWS], U16, name="offs_t")
         lists = [keep.tile([P, V // LIST_ROWS], U16, name=f"list{l}") for l in range(3)]
         w1_raw = keep.tile([P, PACK, H], F32, name="w1_raw")
-        x_rows = keep.tile([P, S], U8, name="x_rows", align_bytes=64)
+        x_rows = keep.tile([P, S], U8, name="x_rows", tag="x_rows", align_bytes=64)
         x_planes = keep.tile([P, S], U8, name="x_planes", align_bytes=64)
-        warm = keep.tile([P, 2], F32, name="warm")
 
-        nc.scalar.dma_start(planes[16:32, :].bitcast(I32), x_scales[0].bitcast(I32))
+        nc.vector.memset(planes[:].bitcast(I32), 0)
+        warm = keep.tile([P, 2], F32, name="warm")
         nc.gpsimd.memset(warm[:, 0:1], 0.0)
         nc.scalar.copy(warm[:, 1:2], warm[:, 0:1])
-        nc.vector.memset(planes[0:16, :].bitcast(I32), 0)
-        nc.vector.memset(planes[32:64, :].bitcast(I32), 0)
-        nc.vector.memset(planes[64:P, :].bitcast(I32), 0)
-        nc.gpsimd.memset(x_planes[:].bitcast(I32), 0)
+        w1_rows = w1.rearrange("(p j) c -> p j c", j=PACK)
+        nc.sync.dma_start(w1_raw[:, :2, :], w1_rows[:, :2, :])
         nc.sync.dma_start(offs_t[:], offs)
-        nc.sync.dma_start(w1_raw[:], w1.rearrange("(p j) c -> p j c", j=PACK))
-        nc.sync.dma_start(lists[0][:], p1)
+        nc.sync.dma_start(planes[0:P:8, :].bitcast(I32), x_scales[0].bitcast(I32))
+        nc.sync.dma_start(w1_raw[:, 2:, :], w1_rows[:, 2:, :])
         nc.sync.dma_start(words[:], x_words[0].rearrange("p n r -> p (n r)").bitcast(I32))
-        nc.sync.dma_start(lists[1][:], p2)
-        nc.sync.dma_start(lists[2][:], p3)
+        for tile, src in zip(lists, (p1, p2, p3)):
+            nc.sync.dma_start(tile[:], src)
         nc.vector.tensor_copy(x_rows[:], planes[:].indirect(offs_t[:]))
-        for q in range(4):
-            nc.scalar.dma_start(x_planes[32 * q : 32 * q + 4, :].bitcast(I32), x_rows[16 + 4 * q : 20 + 4 * q, :].bitcast(I32))
+        nc.vector.tensor_copy(x_planes[:].bitcast(I32), x_rows[:].bitcast(I32))
+        for r in range(1, 4):
+            nc.scalar.dma_start(x_planes[r:P:32, :].bitcast(I32), x_planes[8 * r : P : 32, :].bitcast(I32))
 
-        w1_bf = [keep.tile([P, 2, P, PACK], BF16, name=f"w1_bf{pair}", tag=tag, align_bytes=64) for pair, tag in enumerate(("w1_bf0", "late"))]
+        w1_bf = [keep.tile([P, 2, P, PACK], BF16, name=f"w1_bf{pair}", tag=tag, align_bytes=64) for pair, tag in enumerate(("late", "x_rows"))]
 
         def deal(engine_copy, pair):
             engine_copy(
@@ -69,8 +68,8 @@ def tile_picked_tropic_none_p_kernel(
             )
 
         x_codes = keep.tile([P, S], U32, name="x_codes", align_bytes=64)
-        deal(nc.scalar.copy, 0)
-        deal(nc.vector.tensor_copy, 1)
+        deal(nc.vector.tensor_copy, 0)
+        deal(nc.scalar.copy, 1)
         w1_codes = {}
         w1_planes = keep.tile([P, H], U8, name="w1_planes", align_bytes=64)
 
@@ -81,7 +80,6 @@ def tile_picked_tropic_none_p_kernel(
                 w1_codes[pair][:].bitcast(FP8X4), w1_planes[:, cols], w1_bf[pair][:].rearrange("p t m j -> p (t m j)")
             )
 
-        quantize_w1(1, "w1_codes1")
         quantize_w1(0, "w1_codes0")
 
         late = keep.tile([P, 5 * PACK * V], F32, name="late", tag="late", align_bytes=64)
@@ -107,7 +105,8 @@ def tile_picked_tropic_none_p_kernel(
             picked = slice(h * HALF_S, (h + 1) * HALF_S)
             part = offs_t[:, h * HALF_S // LIST_ROWS : (h + 1) * HALF_S // LIST_ROWS]
             nc.vector.tensor_copy(x_codes[:, picked], words[:].bitcast(U32).indirect(part))
-        w2_bf = keep.tile([P, PACK, P, PACK], BF16, name="w2_bf", tag="words", align_bytes=64)
+        quantize_w1(1, "words")
+        w2_bf = keep.tile([P, N, PACK], BF16, name="w2_bf", tag="words", align_bytes=64)
 
         y = [keep.tile([P, S], F32, name=f"y{t}", tag=f"y{t}", align_bytes=64) for t in range(PACK)]
         pieces = [(0, 0, HALF_S), (1, 0, HALF_S), (0, HALF_S, 3 * S // 4), (0, 3 * S // 4, S), (1, HALF_S, S)]
@@ -143,11 +142,8 @@ def tile_picked_tropic_none_p_kernel(
                 interleave(nc.scalar.copy, tiles[h][:], cand[:, :, states])
             return tiles
 
-        for pair in range(2):
-            nc.scalar.copy(
-                w2_bf[:, 2 * pair : 2 * pair + 2].rearrange("p t (c i) j -> p c j i t", i=2),
-                w2_raw[pair].rearrange("p j (c i t) -> p c j i t", i=2, t=2),
-            )
+        for i in range(2):
+            interleave(nc.scalar.copy, w2_bf[:, w2_cuts[i][0] : w2_cuts[i][1], :], w2_raw[i])
         c1 = rounded(0, candidates(0))
         c2 = rounded(1, candidates(1))
         last = candidates(2)
@@ -176,7 +172,7 @@ def tile_picked_tropic_none_p_kernel(
 
         def quantize_w2(ta, tb, tag):
             codes = keep.tile([P, (tb - ta) * P], U32, name=f"w2_codes{ta}", tag=tag, align_bytes=64)
-            nc.vector.quantize_mx(codes[:].bitcast(FP8X4), w2_planes[:, ta * P : tb * P], w2_bf[:, ta:tb].rearrange("p t m j -> p (t m j)"))
+            nc.vector.quantize_mx(codes[:].bitcast(FP8X4), w2_planes[:, ta * P : tb * P], w2_bf[:, ta * P : tb * P, :].rearrange("p c j -> p (c j)"))
             for t in range(ta, tb):
                 w2_codes[t] = codes[:, (t - ta) * P : (t - ta + 1) * P]
 
@@ -190,7 +186,7 @@ def tile_picked_tropic_none_p_kernel(
         quantize_z(1)
         quantize_w2(3, 4, "late")
 
-        out_rows = out.rearrange("(a p t) v -> a p t v", a=2, t=2)
+        out_rows = out.rearrange("(a t p) v -> a p t v", a=2, t=2)
 
         def project(ta, tb, h, dst, engine_copy):
             acc2 = banks.tile([P, tb - ta, HALF_V], F32, name="acc2", tag="bank")
@@ -206,10 +202,11 @@ def tile_picked_tropic_none_p_kernel(
         project(0, 2, 0, low[0][:], nc.scalar.copy)
         nc.sync.dma_start(out_rows[0][:, :, halves[0]], low[0][:])
         project(2, 3, 0, high[0][:, :, halves[0]], nc.scalar.copy)
-        project(0, 2, 1, low[1][:], nc.vector.tensor_copy)
-        nc.sync.dma_start(out_rows[0][:, :, halves[1]], low[1][:])
         project(2, 3, 1, high[0][:, :, halves[1]], nc.scalar.copy)
         nc.sync.dma_start(out_rows[1][:, 0:1, :], high[0][:])
-        project(3, 4, 0, high[1][:, :, halves[0]], nc.scalar.copy)
-        project(3, 4, 1, high[1][:, :, halves[1]], nc.vector.tensor_copy)
+        project(0, 1, 1, low[1][:, 0:1, :], nc.vector.tensor_copy)
+        project(1, 2, 1, low[1][:, 1:2, :], nc.scalar.copy)
+        nc.sync.dma_start(out_rows[0][:, :, halves[1]], low[1][:])
+        project(3, 4, 0, high[1][:, :, halves[0]], nc.vector.tensor_copy)
+        project(3, 4, 1, high[1][:, :, halves[1]], nc.scalar.copy)
         nc.sync.dma_start(out_rows[1][:, 1:2, :], high[1][:])

@@ -106,7 +106,7 @@ def tile_picked_tropic_none_p_kernel(
             part = offs_t[:, h * HALF_S // LIST_ROWS : (h + 1) * HALF_S // LIST_ROWS]
             nc.vector.tensor_copy(x_codes[:, picked], words[:].bitcast(U32).indirect(part))
         quantize_w1(1, "words")
-        w2_bf = keep.tile([P, N, PACK], BF16, name="w2_bf", tag="words", align_bytes=64)
+        w2_bf = keep.tile([P, 3 * P, PACK], BF16, name="w2_bf", tag="words", align_bytes=64)
 
         y = [keep.tile([P, S], F32, name=f"y{t}", tag=f"y{t}", align_bytes=64) for t in range(PACK)]
         pieces = [(0, 0, HALF_S), (1, 0, HALF_S), (0, HALF_S, 3 * S // 4), (0, 3 * S // 4, S), (1, HALF_S, S)]
@@ -125,7 +125,7 @@ def tile_picked_tropic_none_p_kernel(
         w2_planes = keep.tile([P, N], U8, name="w2_planes", align_bytes=64)
 
         def candidates(l):
-            cand = keep.tile([P, PACK, V], F32, name=f"cand{l}")
+            cand = keep.tile([P, PACK, V], F32, name=f"cand{l}", tag=f"cand{l}", align_bytes=64)
             for t in range(PACK):
                 nc.vector.tensor_tensor(cand[:, t, :], y[t][:].indirect(lists[l][:]), steps[l][:, t, :], ADD)
             return cand
@@ -142,8 +142,8 @@ def tile_picked_tropic_none_p_kernel(
                 interleave(nc.scalar.copy, tiles[h][:], cand[:, :, states])
             return tiles
 
-        for i in range(2):
-            interleave(nc.scalar.copy, w2_bf[:, w2_cuts[i][0] : w2_cuts[i][1], :], w2_raw[i])
+        interleave(nc.scalar.copy, w2_bf[:, : 2 * P, :], w2_raw[0])
+        interleave(nc.scalar.copy, w2_bf[:, 2 * P :, :], w2_raw[1][:, :, :P])
         c1 = rounded(0, candidates(0))
         c2 = rounded(1, candidates(1))
         last = candidates(2)
@@ -151,19 +151,20 @@ def tile_picked_tropic_none_p_kernel(
         interleave(nc.scalar.copy, c3[:, 0], last[:, 0:2, :])
         for states in halves:
             interleave(nc.scalar.copy, c3[:, 1, states, :], last[:, 2:4, states])
-        best = {}
+        w2_last = keep.tile([P, P, PACK], BF16, name="w2_last", tag="cand2", align_bytes=64)
+        interleave(nc.scalar.copy, w2_last[:], w2_raw[1][:, :, P:])
+        best = keep.tile([P, V, PACK], BF16, name="best", tag="y2", align_bytes=64)
         z = [half_tile(f"z{h}", f"z{h}") for h in range(2)]
         z_codes = keep.tile([P, V], U32, name="z_codes", align_bytes=64)
         z_planes = keep.tile([P, V], U8, name="z_planes", align_bytes=64)
         w2_codes = {}
 
-        def best_of_two(h, tag):
-            best[h] = half_tile(f"best{h}", tag)
-            nc.vector.tensor_tensor(best[h][:], c1[h][:], c2[h][:], MAX)
+        def best_of_two(h):
+            nc.vector.tensor_tensor(best[:, halves[h], :], c1[h][:], c2[h][:], MAX)
 
         def best_of_three(h):
             nc.vector.tensor_tensor(
-                z[h][:].rearrange("p v (a j) -> p v a j", a=2), best[h][:].rearrange("p v (a j) -> p v a j", a=2),
+                z[h][:].rearrange("p v (a j) -> p v a j", a=2), best[:, halves[h], :].rearrange("p v (a j) -> p v a j", a=2),
                 c3[:, :, halves[h], :].rearrange("p a v j -> p v a j"), MAX,
             )
 
@@ -172,19 +173,20 @@ def tile_picked_tropic_none_p_kernel(
 
         def quantize_w2(ta, tb, tag):
             codes = keep.tile([P, (tb - ta) * P], U32, name=f"w2_codes{ta}", tag=tag, align_bytes=64)
-            nc.vector.quantize_mx(codes[:].bitcast(FP8X4), w2_planes[:, ta * P : tb * P], w2_bf[:, ta * P : tb * P, :].rearrange("p c j -> p (c j)"))
+            src = w2_last[:] if ta == 3 else w2_bf[:, ta * P : tb * P, :]
+            nc.vector.quantize_mx(codes[:].bitcast(FP8X4), w2_planes[:, ta * P : tb * P], src.rearrange("p c j -> p (c j)"))
             for t in range(ta, tb):
                 w2_codes[t] = codes[:, (t - ta) * P : (t - ta + 1) * P]
 
-        best_of_two(0, "y2")
+        best_of_two(0)
         quantize_w2(0, 2, "y3")
+        best_of_two(1)
         best_of_three(0)
-        best_of_two(1, "late")
-        quantize_z(0)
         best_of_three(1)
-        quantize_w2(2, 3, "z0")
+        quantize_z(0)
+        quantize_w2(2, 3, "y2")
         quantize_z(1)
-        quantize_w2(3, 4, "late")
+        quantize_w2(3, 4, "z0")
 
         out_rows = out.rearrange("(a t p) v -> a p t v", a=2, t=2)
 
@@ -199,8 +201,9 @@ def tile_picked_tropic_none_p_kernel(
 
         low = [keep.tile([P, 2, HALF_V], F32, name=f"low{h}") for h in range(2)]
         high = [keep.tile([P, 1, V], F32, name=f"high{t}") for t in range(2)]
-        project(0, 2, 0, low[0][:], nc.scalar.copy)
-        nc.sync.dma_start(out_rows[0][:, :, halves[0]], low[0][:])
+        for t in range(2):
+            project(t, t + 1, 0, low[0][:, t : t + 1, :], nc.scalar.copy)
+            nc.sync.dma_start(out_rows[0][:, t : t + 1, halves[0]], low[0][:, t : t + 1, :])
         project(2, 3, 0, high[0][:, :, halves[0]], nc.scalar.copy)
         project(2, 3, 1, high[0][:, :, halves[1]], nc.scalar.copy)
         nc.sync.dma_start(out_rows[1][:, 0:1, :], high[0][:])

@@ -106,7 +106,7 @@ def tile_picked_tropic_none_p_kernel(
             part = offs_t[:, h * HALF_S // LIST_ROWS : (h + 1) * HALF_S // LIST_ROWS]
             nc.vector.tensor_copy(x_codes[:, picked], words[:].bitcast(U32).indirect(part))
         quantize_w1(1, "words")
-        w2_bf = keep.tile([P, 3 * P, PACK], BF16, name="w2_bf", tag="words", align_bytes=64)
+        w2_bf = keep.tile([P, N, PACK], BF16, name="w2_bf", tag="words", align_bytes=64)
 
         y = [keep.tile([P, S], F32, name=f"y{t}", tag=f"y{t}", align_bytes=64) for t in range(PACK)]
         pieces = [(0, 0, HALF_S), (1, 0, HALF_S), (0, HALF_S, 3 * S // 4), (0, 3 * S // 4, S), (1, HALF_S, S)]
@@ -136,14 +136,12 @@ def tile_picked_tropic_none_p_kernel(
             return keep.tile([P, HALF_V, PACK], BF16, name=name, tag=tag, align_bytes=64)
 
         def rounded(l, cand):
-            tiles = []
-            for h, states in enumerate(halves):
-                tiles.append(half_tile(f"cand_bf{l}_{h}", f"cand_bf{l}_{h}"))
-                interleave(nc.scalar.copy, tiles[h][:], cand[:, :, states])
-            return tiles
+            tile = keep.tile([P, V, PACK], BF16, name=f"cand_bf{l}", align_bytes=64)
+            interleave(nc.scalar.copy, tile[:], cand[:])
+            return tile
 
-        interleave(nc.scalar.copy, w2_bf[:, : 2 * P, :], w2_raw[0])
-        interleave(nc.scalar.copy, w2_bf[:, 2 * P :, :], w2_raw[1][:, :, :P])
+        for i in range(2):
+            interleave(nc.scalar.copy, w2_bf[:, w2_cuts[i][0] : w2_cuts[i][1], :], w2_raw[i])
         c1 = rounded(0, candidates(0))
         c2 = rounded(1, candidates(1))
         last = candidates(2)
@@ -151,16 +149,11 @@ def tile_picked_tropic_none_p_kernel(
         interleave(nc.scalar.copy, c3[:, 0], last[:, 0:2, :])
         for states in halves:
             interleave(nc.scalar.copy, c3[:, 1, states, :], last[:, 2:4, states])
-        w2_last = keep.tile([P, P, PACK], BF16, name="w2_last", tag="cand2", align_bytes=64)
-        interleave(nc.scalar.copy, w2_last[:], w2_raw[1][:, :, P:])
         best = keep.tile([P, V, PACK], BF16, name="best", tag="y2", align_bytes=64)
         z = [half_tile(f"z{h}", f"z{h}") for h in range(2)]
         z_codes = keep.tile([P, V], U32, name="z_codes", align_bytes=64)
         z_planes = keep.tile([P, V], U8, name="z_planes", align_bytes=64)
         w2_codes = {}
-
-        def best_of_two(h):
-            nc.vector.tensor_tensor(best[:, halves[h], :], c1[h][:], c2[h][:], MAX)
 
         def best_of_three(h):
             nc.vector.tensor_tensor(
@@ -173,14 +166,13 @@ def tile_picked_tropic_none_p_kernel(
 
         def quantize_w2(ta, tb, tag):
             codes = keep.tile([P, (tb - ta) * P], U32, name=f"w2_codes{ta}", tag=tag, align_bytes=64)
-            src = w2_last[:] if ta == 3 else w2_bf[:, ta * P : tb * P, :]
+            src = w2_bf[:, ta * P : tb * P, :]
             nc.vector.quantize_mx(codes[:].bitcast(FP8X4), w2_planes[:, ta * P : tb * P], src.rearrange("p c j -> p (c j)"))
             for t in range(ta, tb):
                 w2_codes[t] = codes[:, (t - ta) * P : (t - ta + 1) * P]
 
-        best_of_two(0)
+        nc.vector.tensor_tensor(best[:], c1[:], c2[:], MAX)
         quantize_w2(0, 2, "y3")
-        best_of_two(1)
         best_of_three(0)
         best_of_three(1)
         quantize_z(0)

@@ -57,9 +57,9 @@ def tile_picked_tropic_none_p_kernel(
         nc.vector.tensor_copy(x_rows[:], planes[:].indirect(offs_t[:]))
         nc.vector.tensor_copy(x_planes[:].bitcast(I32), x_rows[:].bitcast(I32))
         for r in range(1, 4):
-            nc.scalar.dma_start(x_planes[r:P:32, :].bitcast(I32), x_planes[8 * r : P : 32, :].bitcast(I32))
+            nc.sync.dma_start(x_planes[r:P:32, :].bitcast(I32), x_planes[8 * r : P : 32, :].bitcast(I32))
 
-        w1_bf = [keep.tile([P, 2, P, PACK], BF16, name=f"w1_bf{pair}", tag=tag, align_bytes=64) for pair, tag in enumerate(("late", "x_rows"))]
+        w1_bf = [keep.tile([P, 2, P, PACK], BF16, name=f"w1_bf{pair}", tag=tag, align_bytes=64) for pair, tag in enumerate(("w1_bf0", "w1_bf1"))]
 
         def deal(engine_copy, pair):
             engine_copy(
@@ -82,7 +82,7 @@ def tile_picked_tropic_none_p_kernel(
 
         quantize_w1(0, "w1_codes0")
 
-        late = keep.tile([P, 5 * PACK * V], F32, name="late", tag="late", align_bytes=64)
+        late = keep.tile([P, 5 * PACK * V], F32, name="late", tag="x_rows", align_bytes=64)
         steps = [late[:, l * PACK * V : (l + 1) * PACK * V].rearrange("p (j v) -> p j v", j=PACK) for l in range(3)]
         w2_cuts = [(0, 2 * P), (2 * P, N)]
         w2_at = 3 * PACK * V

@@ -20,6 +20,7 @@ PACK = 4
 LIST_ROWS = 16
 HALF_S = S // 2
 HALF_V = V // 2
+STEP_BYTES = 3 * PACK * V * 4
 
 
 def interleave(engine_copy, dst, src):
@@ -32,26 +33,27 @@ def tile_picked_tropic_none_p_kernel(
     nc = tc.nc
     with ExitStack() as ctx:
         keep = ctx.enter_context(tc.tile_pool(name="keep", bufs=1))
+        reused = ctx.enter_context(tc.tile_pool(name="reused", bufs=1))
         banks = ctx.enter_context(tc.psum_pool(name="banks", bufs=8))
 
         words = keep.tile([P, T], I32, name="words", tag="words", align_bytes=64)
         planes = keep.tile([P, T], U8, name="planes", tag="planes", align_bytes=64)
         offs_t = keep.tile([P, S // LIST_ROWS], U16, name="offs_t")
         lists = [keep.tile([P, V // LIST_ROWS], U16, name=f"list{l}") for l in range(3)]
-        w1_raw = keep.tile([P, PACK, H], F32, name="w1_raw")
-        x_rows = keep.tile([P, S], U8, name="x_rows", tag="x_rows", align_bytes=64)
+        w1_raw = [keep.tile([P, 2, H], F32, name=f"w1_raw{a}") for a in range(2)]
+        x_rows = reused.tile([P, S], U8, name="x_rows", align_bytes=64, offset=STEP_BYTES - S // 2)
         x_planes = keep.tile([P, S], U8, name="x_planes", align_bytes=64)
 
-        nc.vector.memset(planes[:].bitcast(I32), 0)
         warm = keep.tile([P, 2], F32, name="warm")
-        nc.gpsimd.memset(warm[:, 0:1], 0.0)
+        nc.vector.memset(warm[:, 0:1], 0.0)
+        nc.vector.memset(planes[:].bitcast(I32), 0)
         nc.scalar.copy(warm[:, 1:2], warm[:, 0:1])
         w1_rows = w1.rearrange("(p j) c -> p j c", j=PACK)
-        nc.sync.dma_start(w1_raw[:, :2, :], w1_rows[:, :2, :])
+        nc.sync.dma_start(w1_raw[0][:], w1_rows[:, :2, :])
         nc.sync.dma_start(offs_t[:], offs)
         nc.sync.dma_start(planes[0:P:8, :].bitcast(I32), x_scales[0].bitcast(I32))
-        nc.sync.dma_start(w1_raw[:, 2:, :], w1_rows[:, 2:, :])
         nc.sync.dma_start(words[:], x_words[0].rearrange("p n r -> p (n r)").bitcast(I32))
+        nc.sync.dma_start(w1_raw[1][:], w1_rows[:, 2:, :])
         for tile, src in zip(lists, (p1, p2, p3)):
             nc.sync.dma_start(tile[:], src)
         nc.vector.tensor_copy(x_rows[:], planes[:].indirect(offs_t[:]))
@@ -59,76 +61,83 @@ def tile_picked_tropic_none_p_kernel(
         for r in range(1, 4):
             nc.sync.dma_start(x_planes[r:P:32, :].bitcast(I32), x_planes[8 * r : P : 32, :].bitcast(I32))
 
-        w1_bf = [keep.tile([P, 2, P, PACK], BF16, name=f"w1_bf{pair}", tag=tag, align_bytes=64) for pair, tag in enumerate(("w1_bf0", "w1_bf1"))]
+        w1_bf = keep.tile([P, PACK, P, PACK], BF16, name="w1_bf", align_bytes=64)
 
-        def deal(engine_copy, pair):
+        def deal(engine_copy, a, t0, t1_, m0, m1):
             engine_copy(
-                w1_bf[pair][:].rearrange("p t m j -> p m j t"),
-                w1_raw[:].rearrange("p j (m t) -> p m j t", t=PACK)[:, :, :, 2 * pair : 2 * pair + 2],
+                w1_bf[:, t0:t1_, m0:m1, 2 * a : 2 * a + 2].rearrange("p t m j -> p m j t"),
+                w1_raw[a][:].rearrange("p j (m t) -> p m j t", t=PACK)[:, m0:m1, :, t0:t1_],
             )
 
         x_codes = keep.tile([P, S], U32, name="x_codes", align_bytes=64)
-        deal(nc.vector.tensor_copy, 0)
-        deal(nc.scalar.copy, 1)
         w1_codes = {}
         w1_planes = keep.tile([P, H], U8, name="w1_planes", align_bytes=64)
 
-        def quantize_w1(pair, tag):
-            cols = slice(pair * 2 * P, (pair + 1) * 2 * P)
-            w1_codes[pair] = keep.tile([P, 2 * P], U32, name=f"w1_codes{pair}", tag=tag, align_bytes=64)
-            nc.vector.quantize_mx(
-                w1_codes[pair][:].bitcast(FP8X4), w1_planes[:, cols], w1_bf[pair][:].rearrange("p t m j -> p (t m j)")
-            )
+        def quantize_w1(ta, tb, tag):
+            cols = slice(ta * P, tb * P)
+            codes = keep.tile([P, (tb - ta) * P], U32, name=f"w1_codes{ta}", tag=tag, align_bytes=64)
+            for t in range(ta, tb):
+                w1_codes[t] = codes[:, (t - ta) * P : (t - ta + 1) * P]
+            nc.vector.quantize_mx(codes[:].bitcast(FP8X4), w1_planes[:, cols], w1_bf[:, ta:tb].rearrange("p t m j -> p (t m j)"))
 
-        quantize_w1(0, "w1_codes0")
+        deal(nc.scalar.copy, 0, 0, PACK, 0, P)
 
-        late = keep.tile([P, 5 * PACK * V], F32, name="late", tag="x_rows", align_bytes=64)
+        late = reused.tile([P, 3 * PACK * V], F32, name="late", align_bytes=64, offset=0)
+        w2_late = reused.tile([P, PACK * N], F32, name="w2_late", align_bytes=64, offset=STEP_BYTES)
         steps = [late[:, l * PACK * V : (l + 1) * PACK * V].rearrange("p (j v) -> p j v", j=PACK) for l in range(3)]
         w2_cuts = [(0, 2 * P), (2 * P, N)]
-        w2_at = 3 * PACK * V
-        w2_raw = [late[:, w2_at + PACK * c0 : w2_at + PACK * c1].rearrange("p (j c) -> p j c", j=PACK) for c0, c1 in w2_cuts]
+        w2_raw = [w2_late[:, PACK * c0 : PACK * c1].rearrange("p (j c) -> p j c", j=PACK) for c0, c1 in w2_cuts]
         w2_rows = w2.rearrange("(p j) c -> p j c", j=PACK)
 
-        def load_step(l, t):
-            nc.sync.dma_start(steps[l], t.rearrange("(p j) v -> p j v", j=PACK))
+        def load_step(l, t, rows=slice(0, PACK)):
+            nc.sync.dma_start(steps[l][:, rows, :], t.rearrange("(p j) v -> p j v", j=PACK)[:, rows, :])
 
         def load_w2(i):
             nc.sync.dma_start(w2_raw[i], w2_rows[:, :, w2_cuts[i][0] : w2_cuts[i][1]])
 
-        load_step(0, t1)
+        load_step(0, t1, slice(0, 2))
+        load_step(1, t2, slice(0, 2))
+        load_step(0, t1, slice(2, PACK))
         load_w2(0)
-        load_step(1, t2)
         load_w2(1)
+        load_step(1, t2, slice(2, PACK))
         load_step(2, t3)
 
         for h in range(2):
             picked = slice(h * HALF_S, (h + 1) * HALF_S)
             part = offs_t[:, h * HALF_S // LIST_ROWS : (h + 1) * HALF_S // LIST_ROWS]
             nc.vector.tensor_copy(x_codes[:, picked], words[:].bitcast(U32).indirect(part))
-        quantize_w1(1, "words")
+        deal(nc.scalar.copy, 1, 0, 1, 0, P // 2)
+        deal(nc.vector.tensor_copy, 1, 0, 1, P // 2, P)
+        deal(nc.vector.tensor_copy, 1, 1, 2, 0, P)
+        quantize_w1(0, 1, "w1_codes0")
+        deal(nc.scalar.copy, 1, 2, 3, 0, P)
+        deal(nc.scalar.copy, 1, 3, 4, 0, P)
+        quantize_w1(1, 2, "w1_codes1")
+        quantize_w1(2, 3, "w1_codes2")
         w2_bf = keep.tile([P, N, PACK], BF16, name="w2_bf", tag="words", align_bytes=64)
 
         y = [keep.tile([P, S], F32, name=f"y{t}", tag=f"y{t}", align_bytes=64) for t in range(PACK)]
-        pieces = [(0, 0, HALF_S), (1, 0, HALF_S), (0, HALF_S, 3 * S // 4), (0, 3 * S // 4, S), (1, HALF_S, S)]
-        pieces = pieces + [(2, 0, S), (3, 0, S)]
+        pieces = [(0, 0, HALF_S), (0, HALF_S, 3 * S // 4), (0, 3 * S // 4, S), (1, 0, S), (2, 0, S), (3, 0, S)]
         for t, s0, s1 in pieces:
+            if (t, s0) == (1, 0):
+                quantize_w1(3, 4, "w1_codes0")
             cols = slice(t * P, (t + 1) * P)
             picked = slice(s0, s1)
             acc = banks.tile([P, s1 - s0], F32, name="acc", tag="bank")
             nc.tensor.matmul_mx(
-                acc[:], w1_codes[t // 2][:, (t % 2) * P : (t % 2 + 1) * P].bitcast(FP8X4), w1_planes[:, cols],
+                acc[:], w1_codes[t].bitcast(FP8X4), w1_planes[:, cols],
                 x_codes[:, picked].bitcast(FP8X4), x_planes[:, picked], start=True, stop=True,
             )
-            engine_copy = nc.vector.tensor_copy if (t, s0) == (1, 0) else nc.scalar.copy
+            engine_copy = nc.vector.tensor_copy if (t, s0) == (0, 0) else nc.scalar.copy
             engine_copy(y[t][:, picked], acc[:])
 
         w2_planes = keep.tile([P, N], U8, name="w2_planes", align_bytes=64)
 
-        def candidates(l):
-            cand = keep.tile([P, PACK, V], F32, name=f"cand{l}", tag=f"cand{l}", align_bytes=64)
-            for t in range(PACK):
-                nc.vector.tensor_tensor(cand[:, t, :], y[t][:].indirect(lists[l][:]), steps[l][:, t, :], ADD)
-            return cand
+        cands = [keep.tile([P, PACK, V], F32, name=f"cand{l}", tag=f"cand{l}", align_bytes=64) for l in range(3)]
+
+        def candidate(l, t):
+            nc.vector.tensor_tensor(cands[l][:, t, :], y[t][:].indirect(lists[l][:]), steps[l][:, t, :], ADD)
 
         halves = [slice(h * HALF_V, (h + 1) * HALF_V) for h in range(2)]
 
@@ -136,15 +145,23 @@ def tile_picked_tropic_none_p_kernel(
             return keep.tile([P, HALF_V, PACK], BF16, name=name, tag=tag, align_bytes=64)
 
         def rounded(l, cand):
-            tile = keep.tile([P, V, PACK], BF16, name=f"cand_bf{l}", align_bytes=64)
+            tile = reused.tile([P, V, PACK], BF16, name=f"cand_bf{l}", align_bytes=64, offset=STEP_BYTES + (l + 1) * V * PACK * 2)
             interleave(nc.scalar.copy, tile[:], cand[:])
             return tile
 
         for i in range(2):
             interleave(nc.scalar.copy, w2_bf[:, w2_cuts[i][0] : w2_cuts[i][1], :], w2_raw[i])
-        c1 = rounded(0, candidates(0))
-        c2 = rounded(1, candidates(1))
-        last = candidates(2)
+        for t in range(2):
+            candidate(0, t)
+            candidate(1, t)
+        for l in range(2):
+            candidate(l, 2)
+            candidate(l, 3)
+        c1 = rounded(0, cands[0])
+        c2 = rounded(1, cands[1])
+        for t in range(PACK):
+            candidate(2, t)
+        last = cands[2]
         c3 = keep.tile([P, 2, V, 2], BF16, name="c3", align_bytes=64)
         interleave(nc.scalar.copy, c3[:, 0], last[:, 0:2, :])
         for states in halves:
@@ -172,7 +189,7 @@ def tile_picked_tropic_none_p_kernel(
                 w2_codes[t] = codes[:, (t - ta) * P : (t - ta + 1) * P]
 
         nc.vector.tensor_tensor(best[:], c1[:], c2[:], MAX)
-        quantize_w2(0, 2, "y3")
+        quantize_w2(0, 2, "cand1")
         best_of_three(0)
         best_of_three(1)
         quantize_z(0)

@@ -14,17 +14,21 @@ U8 = mybir.dt.uint8
 FP8X4 = mybir.dt.float8_e4m3fn_x4
 ADD = mybir.AluOpType.add
 MAX = mybir.AluOpType.max
+COPY = mybir.ActivationFunctionType.Copy
 
 P = 128
 PACK = 4
 LIST_ROWS = 16
 HALF_S = S // 2
 HALF_V = V // 2
-STEP_BYTES = 3 * PACK * V * 4
 
 
-def interleave(engine_copy, dst, src):
-    engine_copy(dst.rearrange("p (c i) j -> p c j i", i=4), src.rearrange("p j (c i) -> p c j i", i=4))
+def woven(ap):
+    return ap.rearrange("p (c i) j -> p c j i", i=4)
+
+
+def planar(ap):
+    return ap.rearrange("p j (c i) -> p c j i", i=4)
 
 
 def tile_picked_tropic_none_p_kernel(
@@ -36,12 +40,12 @@ def tile_picked_tropic_none_p_kernel(
         reused = ctx.enter_context(tc.tile_pool(name="reused", bufs=1))
         banks = ctx.enter_context(tc.psum_pool(name="banks", bufs=8))
 
-        words = keep.tile([P, T], I32, name="words", tag="words", align_bytes=64)
-        planes = keep.tile([P, T], U8, name="planes", tag="planes", align_bytes=64)
+        words = keep.tile([P, T], I32, name="words", align_bytes=64)
+        planes = keep.tile([P, T], U8, name="planes", align_bytes=64)
         offs_t = keep.tile([P, S // LIST_ROWS], U16, name="offs_t")
         lists = [keep.tile([P, V // LIST_ROWS], U16, name=f"list{l}") for l in range(3)]
         w1_raw = [keep.tile([P, 2, H], F32, name=f"w1_raw{a}") for a in range(2)]
-        x_rows = reused.tile([P, S], U8, name="x_rows", align_bytes=64, offset=STEP_BYTES - S // 2)
+        x_rows = reused.tile([P, S], U8, name="x_rows", align_bytes=64, offset=0)
         x_planes = keep.tile([P, S], U8, name="x_planes", align_bytes=64)
 
         warm = keep.tile([P, 2], F32, name="warm")
@@ -82,12 +86,13 @@ def tile_picked_tropic_none_p_kernel(
 
         deal(nc.scalar.copy, 0, 0, PACK, 0, P)
 
-        late = reused.tile([P, 3 * PACK * V], F32, name="late", align_bytes=64, offset=0)
-        w2_late = reused.tile([P, PACK * N], F32, name="w2_late", align_bytes=64, offset=STEP_BYTES)
+        late = reused.tile([P, 3 * PACK * V + PACK * N], F32, name="late", align_bytes=64, offset=0)
         steps = [late[:, l * PACK * V : (l + 1) * PACK * V].rearrange("p (j v) -> p j v", j=PACK) for l in range(3)]
+        w2_late = late[:, 3 * PACK * V :]
         w2_cuts = [(0, 2 * P), (2 * P, N)]
         w2_raw = [w2_late[:, PACK * c0 : PACK * c1].rearrange("p (j c) -> p j c", j=PACK) for c0, c1 in w2_cuts]
         w2_rows = w2.rearrange("(p j) c -> p j c", j=PACK)
+        pairs = [slice(0, 2), slice(2, PACK)]
 
         def load_step(l, t, rows=slice(0, PACK)):
             nc.sync.dma_start(steps[l][:, rows, :], t.rearrange("(p j) v -> p j v", j=PACK)[:, rows, :])
@@ -95,12 +100,12 @@ def tile_picked_tropic_none_p_kernel(
         def load_w2(i):
             nc.sync.dma_start(w2_raw[i], w2_rows[:, :, w2_cuts[i][0] : w2_cuts[i][1]])
 
-        load_step(0, t1, slice(0, 2))
-        load_step(1, t2, slice(0, 2))
-        load_step(0, t1, slice(2, PACK))
         load_w2(0)
+        load_step(0, t1, pairs[0])
+        load_step(1, t2, pairs[0])
         load_w2(1)
-        load_step(1, t2, slice(2, PACK))
+        load_step(0, t1, pairs[1])
+        load_step(1, t2, pairs[1])
         load_step(2, t3)
 
         for h in range(2):
@@ -115,7 +120,6 @@ def tile_picked_tropic_none_p_kernel(
         deal(nc.scalar.copy, 1, 3, 4, 0, P)
         quantize_w1(1, 2, "w1_codes1")
         quantize_w1(2, 3, "w1_codes2")
-        w2_bf = keep.tile([P, N, PACK], BF16, name="w2_bf", tag="words", align_bytes=64)
 
         y = [keep.tile([P, S], F32, name=f"y{t}", tag=f"y{t}", align_bytes=64) for t in range(PACK)]
         pieces = [(0, 0, HALF_S), (0, HALF_S, 3 * S // 4), (0, 3 * S // 4, S), (1, 0, S), (2, 0, S), (3, 0, S)]
@@ -132,93 +136,95 @@ def tile_picked_tropic_none_p_kernel(
             engine_copy = nc.vector.tensor_copy if (t, s0) == (0, 0) else nc.scalar.copy
             engine_copy(y[t][:, picked], acc[:])
 
+        w2_bf = keep.tile([P, N, PACK], BF16, name="w2_bf", align_bytes=64)
         w2_planes = keep.tile([P, N], U8, name="w2_planes", align_bytes=64)
+        w2_all = keep.tile([P, N], U32, name="w2_all", align_bytes=64)
 
-        cands = [keep.tile([P, PACK, V], F32, name=f"cand{l}", tag=f"cand{l}", align_bytes=64) for l in range(3)]
+        def weave_w2(t):
+            i, c0 = divmod(t * P, 2 * P)
+            nc.vector.tensor_copy(woven(w2_bf[:, t * P : (t + 1) * P, :]), planar(w2_raw[i][:, :, c0 : c0 + P]))
 
-        def candidate(l, t):
-            nc.vector.tensor_tensor(cands[l][:, t, :], y[t][:].indirect(lists[l][:]), steps[l][:, t, :], ADD)
+        def quantize_w2(ta, tb):
+            cols = slice(ta * P, tb * P)
+            nc.vector.quantize_mx(w2_all[:, cols].bitcast(FP8X4), w2_planes[:, cols], w2_bf[:, cols, :].rearrange("p c j -> p (c j)"))
 
+        looked = [keep.tile([P, PACK, V], F32, name=f"looked{l}", align_bytes=64) for l in range(3)]
         halves = [slice(h * HALF_V, (h + 1) * HALF_V) for h in range(2)]
+        whole = slice(0, V)
 
-        def half_tile(name, tag):
-            return keep.tile([P, HALF_V, PACK], BF16, name=name, tag=tag, align_bytes=64)
+        def entries(l, states):
+            return lists[l][:, states.start // LIST_ROWS : states.stop // LIST_ROWS]
 
-        def rounded(l, cand):
-            tile = reused.tile([P, V, PACK], BF16, name=f"cand_bf{l}", align_bytes=64, offset=STEP_BYTES + (l + 1) * V * PACK * 2)
-            interleave(nc.scalar.copy, tile[:], cand[:])
-            return tile
+        def fetch_and_add(l, t):
+            nc.vector.tensor_tensor(looked[l][:, t, :], y[t][:].indirect(lists[l][:]), steps[l][:, t, :], ADD)
 
-        for i in range(2):
-            interleave(nc.scalar.copy, w2_bf[:, w2_cuts[i][0] : w2_cuts[i][1], :], w2_raw[i])
-        for t in range(2):
-            candidate(0, t)
-            candidate(1, t)
-        for l in range(2):
-            candidate(l, 2)
-            candidate(l, 3)
-        c1 = rounded(0, cands[0])
-        c2 = rounded(1, cands[1])
-        for t in range(PACK):
-            candidate(2, t)
-        last = cands[2]
-        c3 = keep.tile([P, 2, V, 2], BF16, name="c3", align_bytes=64)
-        interleave(nc.scalar.copy, c3[:, 0], last[:, 0:2, :])
-        for states in halves:
-            interleave(nc.scalar.copy, c3[:, 1, states, :], last[:, 2:4, states])
-        best = keep.tile([P, V, PACK], BF16, name="best", tag="y2", align_bytes=64)
-        z = [half_tile(f"z{h}", f"z{h}") for h in range(2)]
+        def fetch(l, t, states):
+            nc.scalar.activation(looked[l][:, t, states], y[t][:].indirect(entries(l, states)), COPY)
+
+        def add_rounded(dst, l, a, states):
+            nc.vector.tensor_tensor(woven(dst), planar(looked[l][:, pairs[a], states]), planar(steps[l][:, pairs[a], states]), ADD)
+
+        best = keep.tile([P, 2, V, 2], BF16, name="best", align_bytes=64)
+        third = keep.tile([P, 2, V, 2], BF16, name="third", align_bytes=64)
+        sums = [keep.tile([P, V, 2], BF16, name=f"sums{l}", align_bytes=64) for l in range(2)]
+        z = [keep.tile([P, HALF_V, PACK], BF16, name=f"z{h}", align_bytes=64) for h in range(2)]
         z_codes = keep.tile([P, V], U32, name="z_codes", align_bytes=64)
         z_planes = keep.tile([P, V], U8, name="z_planes", align_bytes=64)
-        w2_codes = {}
 
         def best_of_three(h):
             nc.vector.tensor_tensor(
-                z[h][:].rearrange("p v (a j) -> p v a j", a=2), best[:, halves[h], :].rearrange("p v (a j) -> p v a j", a=2),
-                c3[:, :, halves[h], :].rearrange("p a v j -> p v a j"), MAX,
+                z[h][:].rearrange("p v (a j) -> p v a j", a=2), best[:, :, halves[h], :].rearrange("p a v j -> p v a j"),
+                third[:, :, halves[h], :].rearrange("p a v j -> p v a j"), MAX,
             )
 
         def quantize_z(h):
             nc.vector.quantize_mx(z_codes[:, halves[h]].bitcast(FP8X4), z_planes[:, halves[h]], z[h][:].rearrange("p v j -> p (v j)"))
 
-        def quantize_w2(ta, tb, tag):
-            codes = keep.tile([P, (tb - ta) * P], U32, name=f"w2_codes{ta}", tag=tag, align_bytes=64)
-            src = w2_bf[:, ta * P : tb * P, :]
-            nc.vector.quantize_mx(codes[:].bitcast(FP8X4), w2_planes[:, ta * P : tb * P], src.rearrange("p c j -> p (c j)"))
-            for t in range(ta, tb):
-                w2_codes[t] = codes[:, (t - ta) * P : (t - ta + 1) * P]
+        for l in range(2):
+            for t in (2, 3):
+                fetch(l, t, whole)
+        for t in (0, 1):
+            fetch(2, t, whole)
+        for states in halves:
+            for t in (2, 3):
+                fetch(2, t, states)
 
-        nc.vector.tensor_tensor(best[:], c1[:], c2[:], MAX)
-        quantize_w2(0, 2, "cand1")
+        weave_w2(0)
+        weave_w2(1)
+        for t in range(2):
+            fetch_and_add(0, t)
+            fetch_and_add(1, t)
+        quantize_w2(0, 2)
+        nc.vector.tensor_tensor(woven(best[:, 0]), planar(looked[0][:, pairs[0], :]), planar(looked[1][:, pairs[0], :]), MAX)
+        weave_w2(2)
+        weave_w2(3)
+        add_rounded(sums[0][:], 0, 1, whole)
+        add_rounded(sums[1][:], 1, 1, whole)
+        add_rounded(third[:, 0], 2, 0, whole)
+        nc.vector.tensor_tensor(best[:, 1], sums[0][:], sums[1][:], MAX)
+        add_rounded(third[:, 1, halves[0], :], 2, 1, halves[0])
+        quantize_w2(2, 3)
         best_of_three(0)
-        best_of_three(1)
+        add_rounded(third[:, 1, halves[1], :], 2, 1, halves[1])
         quantize_z(0)
-        quantize_w2(2, 3, "y2")
+        best_of_three(1)
+        quantize_w2(3, 4)
         quantize_z(1)
-        quantize_w2(3, 4, "z0")
 
         out_rows = out.rearrange("(a t p) v -> a p t v", a=2, t=2)
 
-        def project(ta, tb, h, dst, engine_copy):
-            acc2 = banks.tile([P, tb - ta, HALF_V], F32, name="acc2", tag="bank")
-            for t in range(ta, tb):
-                nc.tensor.matmul_mx(
-                    acc2[:, t - ta, :], w2_codes[t].bitcast(FP8X4), w2_planes[:, t * P : (t + 1) * P],
-                    z_codes[:, halves[h]].bitcast(FP8X4), z_planes[:, halves[h]], start=True, stop=True,
-                )
+        def project(t, h, dst, engine_copy):
+            acc2 = banks.tile([P, 1, HALF_V], F32, name="acc2", tag="bank")
+            nc.tensor.matmul_mx(
+                acc2[:, 0, :], w2_all[:, t * P : (t + 1) * P].bitcast(FP8X4), w2_planes[:, t * P : (t + 1) * P],
+                z_codes[:, halves[h]].bitcast(FP8X4), z_planes[:, halves[h]], start=True, stop=True,
+            )
             engine_copy(dst, acc2[:])
 
-        low = [keep.tile([P, 2, HALF_V], F32, name=f"low{h}") for h in range(2)]
-        high = [keep.tile([P, 1, V], F32, name=f"high{t}") for t in range(2)]
-        for t in range(2):
-            project(t, t + 1, 0, low[0][:, t : t + 1, :], nc.scalar.copy)
-            nc.sync.dma_start(out_rows[0][:, t : t + 1, halves[0]], low[0][:, t : t + 1, :])
-        project(2, 3, 0, high[0][:, :, halves[0]], nc.scalar.copy)
-        project(2, 3, 1, high[0][:, :, halves[1]], nc.scalar.copy)
-        nc.sync.dma_start(out_rows[1][:, 0:1, :], high[0][:])
-        project(0, 1, 1, low[1][:, 0:1, :], nc.vector.tensor_copy)
-        project(1, 2, 1, low[1][:, 1:2, :], nc.scalar.copy)
-        nc.sync.dma_start(out_rows[0][:, :, halves[1]], low[1][:])
-        project(3, 4, 0, high[1][:, :, halves[0]], nc.vector.tensor_copy)
-        project(3, 4, 1, high[1][:, :, halves[1]], nc.scalar.copy)
-        nc.sync.dma_start(out_rows[1][:, 1:2, :], high[1][:])
+        staged = [[keep.tile([P, 2, HALF_V], F32, name=f"staged{h}{a}") for a in range(2)] for h in range(2)]
+        for h in range(2):
+            for a in range(2):
+                for j in range(2):
+                    engine_copy = nc.vector.tensor_copy if (h, j) == (1, 1) else nc.scalar.copy
+                    project(2 * a + j, h, staged[h][a][:, j : j + 1, :], engine_copy)
+                nc.sync.dma_start(out_rows[a][:, :, halves[h]], staged[h][a][:])

@@ -103,10 +103,10 @@ def tile_picked_tropic_none_p_kernel(
         load_w2(0)
         load_step(0, t1, pairs[0])
         load_step(1, t2, pairs[0])
-        load_w2(1)
         load_step(0, t1, pairs[1])
         load_step(1, t2, pairs[1])
         load_step(2, t3)
+        load_w2(1)
 
         for h in range(2):
             picked = slice(h * HALF_S, (h + 1) * HALF_S)
@@ -140,9 +140,9 @@ def tile_picked_tropic_none_p_kernel(
         w2_planes = keep.tile([P, N], U8, name="w2_planes", align_bytes=64)
         w2_all = keep.tile([P, N], U32, name="w2_all", align_bytes=64)
 
-        def weave_w2(t):
+        def weave_w2(engine_copy, t):
             i, c0 = divmod(t * P, 2 * P)
-            nc.vector.tensor_copy(woven(w2_bf[:, t * P : (t + 1) * P, :]), planar(w2_raw[i][:, :, c0 : c0 + P]))
+            engine_copy(woven(w2_bf[:, t * P : (t + 1) * P, :]), planar(w2_raw[i][:, :, c0 : c0 + P]))
 
         def quantize_w2(ta, tb):
             cols = slice(ta * P, tb * P)
@@ -166,7 +166,7 @@ def tile_picked_tropic_none_p_kernel(
 
         best = keep.tile([P, 2, V, 2], BF16, name="best", align_bytes=64)
         third = keep.tile([P, 2, V, 2], BF16, name="third", align_bytes=64)
-        sums = [keep.tile([P, V, 2], BF16, name=f"sums{l}", align_bytes=64) for l in range(2)]
+        second = keep.tile([P, V, 2], BF16, name="second", align_bytes=64)
         z = [keep.tile([P, HALF_V, PACK], BF16, name=f"z{h}", align_bytes=64) for h in range(2)]
         z_codes = keep.tile([P, V], U32, name="z_codes", align_bytes=64)
         z_planes = keep.tile([P, V], U8, name="z_planes", align_bytes=64)
@@ -180,51 +180,51 @@ def tile_picked_tropic_none_p_kernel(
         def quantize_z(h):
             nc.vector.quantize_mx(z_codes[:, halves[h]].bitcast(FP8X4), z_planes[:, halves[h]], z[h][:].rearrange("p v j -> p (v j)"))
 
-        for l in range(2):
-            for t in (2, 3):
-                fetch(l, t, whole)
-        for t in (0, 1):
+        for t in (2, 3):
+            fetch(1, t, whole)
+        for t in range(PACK):
             fetch(2, t, whole)
-        for states in halves:
-            for t in (2, 3):
-                fetch(2, t, states)
+        weave_w2(nc.scalar.copy, 2)
+        weave_w2(nc.scalar.copy, 3)
 
-        weave_w2(0)
-        weave_w2(1)
+        weave_w2(nc.vector.tensor_copy, 0)
+        weave_w2(nc.vector.tensor_copy, 1)
         for t in range(2):
             fetch_and_add(0, t)
             fetch_and_add(1, t)
         quantize_w2(0, 2)
+        fetch_and_add(0, 2)
+        fetch_and_add(0, 3)
+        add_rounded(second[:], 1, 1, whole)
         nc.vector.tensor_tensor(woven(best[:, 0]), planar(looked[0][:, pairs[0], :]), planar(looked[1][:, pairs[0], :]), MAX)
-        weave_w2(2)
-        weave_w2(3)
-        add_rounded(sums[0][:], 0, 1, whole)
-        add_rounded(sums[1][:], 1, 1, whole)
         add_rounded(third[:, 0], 2, 0, whole)
-        nc.vector.tensor_tensor(best[:, 1], sums[0][:], sums[1][:], MAX)
-        add_rounded(third[:, 1, halves[0], :], 2, 1, halves[0])
+        nc.vector.tensor_tensor(woven(best[:, 1]), planar(looked[0][:, pairs[1], :]), woven(second[:]), MAX)
+        for states in halves:
+            add_rounded(third[:, 1, states, :], 2, 1, states)
+        for h in range(2):
+            best_of_three(h)
+        for h in range(2):
+            quantize_z(h)
         quantize_w2(2, 3)
-        best_of_three(0)
-        add_rounded(third[:, 1, halves[1], :], 2, 1, halves[1])
-        quantize_z(0)
-        best_of_three(1)
         quantize_w2(3, 4)
-        quantize_z(1)
 
         out_rows = out.rearrange("(a t p) v -> a p t v", a=2, t=2)
 
-        def project(t, h, dst, engine_copy):
-            acc2 = banks.tile([P, 1, HALF_V], F32, name="acc2", tag="bank")
+        def project(t, states, dst, engine_copy):
+            acc2 = banks.tile([P, 1, states.stop - states.start], F32, name="acc2", tag="bank")
             nc.tensor.matmul_mx(
                 acc2[:, 0, :], w2_all[:, t * P : (t + 1) * P].bitcast(FP8X4), w2_planes[:, t * P : (t + 1) * P],
-                z_codes[:, halves[h]].bitcast(FP8X4), z_planes[:, halves[h]], start=True, stop=True,
+                z_codes[:, states].bitcast(FP8X4), z_planes[:, states], start=True, stop=True,
             )
             engine_copy(dst, acc2[:])
 
-        staged = [[keep.tile([P, 2, HALF_V], F32, name=f"staged{h}{a}") for a in range(2)] for h in range(2)]
+        low = [keep.tile([P, 2, HALF_V], F32, name=f"low{h}") for h in range(2)]
+        high = [keep.tile([P, 1, V], F32, name=f"high{t}") for t in range(2)]
         for h in range(2):
-            for a in range(2):
-                for j in range(2):
-                    engine_copy = nc.vector.tensor_copy if (h, j) == (1, 1) else nc.scalar.copy
-                    project(2 * a + j, h, staged[h][a][:, j : j + 1, :], engine_copy)
-                nc.sync.dma_start(out_rows[a][:, :, halves[h]], staged[h][a][:])
+            for t in range(2):
+                project(t, halves[h], low[h][:, t : t + 1, :], nc.scalar.copy)
+            nc.sync.dma_start(out_rows[0][:, :, halves[h]], low[h][:])
+        for t in range(2):
+            for h in range(2):
+                project(2 + t, halves[h], high[t][:, :, halves[h]], nc.scalar.copy if h else nc.vector.tensor_copy)
+            nc.sync.dma_start(out_rows[1][:, t : t + 1, :], high[t][:])

@@ -73,7 +73,7 @@ def tile_picked_tropic_none_p_kernel(
                 w1_raw[a][:].rearrange("p j (m t) -> p m j t", t=PACK)[:, m0:m1, :, t0:t1_],
             )
 
-        x_codes = keep.tile([P, S], U32, name="x_codes", align_bytes=64)
+        x_codes = keep.tile([P, S], U32, name="x_codes", tag="codes", align_bytes=64)
         w1_codes = {}
         w1_planes = keep.tile([P, H], U8, name="w1_planes", align_bytes=64)
 
@@ -122,7 +122,7 @@ def tile_picked_tropic_none_p_kernel(
         quantize_w1(2, 3, "w1_codes2")
 
         y = [keep.tile([P, S], F32, name=f"y{t}", tag=f"y{t}", align_bytes=64) for t in range(PACK)]
-        pieces = [(0, 0, HALF_S), (0, HALF_S, 3 * S // 4), (0, 3 * S // 4, S), (1, 0, S), (2, 0, S), (3, 0, S)]
+        pieces = [(0, 0, HALF_S), (0, HALF_S, S), (1, 0, S), (2, 0, S), (3, 0, S)]
         for t, s0, s1 in pieces:
             if (t, s0) == (1, 0):
                 quantize_w1(3, 4, "w1_codes0")
@@ -138,7 +138,7 @@ def tile_picked_tropic_none_p_kernel(
 
         w2_bf = keep.tile([P, N, PACK], BF16, name="w2_bf", align_bytes=64)
         w2_planes = keep.tile([P, N], U8, name="w2_planes", align_bytes=64)
-        w2_all = keep.tile([P, N], U32, name="w2_all", align_bytes=64)
+        w2_all = keep.tile([P, N], U32, name="w2_all", tag="codes", align_bytes=64)
 
         def weave_w2(engine_copy, t):
             i, c0 = divmod(t * P, 2 * P)
@@ -184,8 +184,6 @@ def tile_picked_tropic_none_p_kernel(
             fetch(1, t, whole)
         for t in range(PACK):
             fetch(2, t, whole)
-        weave_w2(nc.scalar.copy, 2)
-        weave_w2(nc.scalar.copy, 3)
 
         weave_w2(nc.vector.tensor_copy, 0)
         weave_w2(nc.vector.tensor_copy, 1)
@@ -195,12 +193,16 @@ def tile_picked_tropic_none_p_kernel(
         quantize_w2(0, 2)
         fetch_and_add(0, 2)
         fetch_and_add(0, 3)
+        first = keep.tile([P, V, 2], BF16, name="first", tag="y2", align_bytes=64)
+        nc.scalar.copy(woven(first[:]), planar(looked[0][:, pairs[1], :]))
+        weave_w2(nc.scalar.copy, 2)
+        weave_w2(nc.scalar.copy, 3)
         add_rounded(second[:], 1, 1, whole)
         nc.vector.tensor_tensor(woven(best[:, 0]), planar(looked[0][:, pairs[0], :]), planar(looked[1][:, pairs[0], :]), MAX)
         add_rounded(third[:, 0], 2, 0, whole)
-        nc.vector.tensor_tensor(woven(best[:, 1]), planar(looked[0][:, pairs[1], :]), woven(second[:]), MAX)
-        for states in halves:
-            add_rounded(third[:, 1, states, :], 2, 1, states)
+        add_rounded(third[:, 1, halves[0], :], 2, 1, halves[0])
+        nc.vector.tensor_tensor(best[:, 1], first[:], second[:], MAX)
+        add_rounded(third[:, 1, halves[1], :], 2, 1, halves[1])
         for h in range(2):
             best_of_three(h)
         for h in range(2):

@@ -21,6 +21,7 @@ PACK = 4
 LIST_ROWS = 16
 HALF_S = S // 2
 HALF_V = V // 2
+FIRST_LOAD = 768
 
 
 def woven(ap):
@@ -53,24 +54,28 @@ def tile_picked_tropic_none_p_kernel(
         nc.vector.memset(planes[:].bitcast(I32), 0)
         nc.scalar.copy(warm[:, 1:2], warm[:, 0:1])
         w1_rows = w1.rearrange("(p j) c -> p j c", j=PACK)
-        nc.sync.dma_start(w1_raw[0][:], w1_rows[:, :2, :])
+        x_rows_hbm = x_words[0].rearrange("p n r -> p (n r)").bitcast(I32)
+        nc.sync.dma_start(words[:, :FIRST_LOAD], x_rows_hbm[:, :FIRST_LOAD])
         nc.sync.dma_start(offs_t[:], offs)
+        nc.sync.dma_start(lists[0][:], p1)
         nc.sync.dma_start(planes[0:P:8, :].bitcast(I32), x_scales[0].bitcast(I32))
-        nc.sync.dma_start(words[:], x_words[0].rearrange("p n r -> p (n r)").bitcast(I32))
+        nc.sync.dma_start(words[:, FIRST_LOAD:], x_rows_hbm[:, FIRST_LOAD:])
+        nc.sync.dma_start(w1_raw[0][:], w1_rows[:, :2, :])
         nc.sync.dma_start(w1_raw[1][:], w1_rows[:, 2:, :])
-        for tile, src in zip(lists, (p1, p2, p3)):
-            nc.sync.dma_start(tile[:], src)
+        nc.sync.dma_start(lists[1][:], p2)
+        nc.sync.dma_start(lists[2][:], p3)
         nc.vector.tensor_copy(x_rows[:], planes[:].indirect(offs_t[:]))
         nc.vector.tensor_copy(x_planes[:].bitcast(I32), x_rows[:].bitcast(I32))
         for r in range(1, 4):
             nc.sync.dma_start(x_planes[r:P:32, :].bitcast(I32), x_planes[8 * r : P : 32, :].bitcast(I32))
 
-        w1_bf = keep.tile([P, PACK, P, PACK], BF16, name="w1_bf", align_bytes=64)
+        w1_bf = [keep.tile([P, 2, P, PACK], BF16, name=f"w1_bf{b}", align_bytes=64) for b in range(2)]
 
-        def deal(engine_copy, a, t0, t1_, m0, m1):
+        def deal(engine_copy, a, t0, t1_):
+            b = t0 // 2
             engine_copy(
-                w1_bf[:, t0:t1_, m0:m1, 2 * a : 2 * a + 2].rearrange("p t m j -> p m j t"),
-                w1_raw[a][:].rearrange("p j (m t) -> p m j t", t=PACK)[:, m0:m1, :, t0:t1_],
+                w1_bf[b][:, t0 - 2 * b : t1_ - 2 * b, :, 2 * a : 2 * a + 2].rearrange("p t m j -> p m j t"),
+                w1_raw[a][:].rearrange("p j (m t) -> p m j t", t=PACK)[:, :, :, t0:t1_],
             )
 
         x_codes = keep.tile([P, S], U32, name="x_codes", tag="codes", align_bytes=64)
@@ -82,9 +87,7 @@ def tile_picked_tropic_none_p_kernel(
             codes = keep.tile([P, (tb - ta) * P], U32, name=f"w1_codes{ta}", tag=tag, align_bytes=64)
             for t in range(ta, tb):
                 w1_codes[t] = codes[:, (t - ta) * P : (t - ta + 1) * P]
-            nc.vector.quantize_mx(codes[:].bitcast(FP8X4), w1_planes[:, cols], w1_bf[:, ta:tb].rearrange("p t m j -> p (t m j)"))
-
-        deal(nc.scalar.copy, 0, 0, PACK, 0, P)
+            nc.vector.quantize_mx(codes[:].bitcast(FP8X4), w1_planes[:, cols], w1_bf[ta // 2][:, ta % 2 : ta % 2 + tb - ta].rearrange("p t m j -> p (t m j)"))
 
         late = reused.tile([P, 3 * PACK * V + PACK * N], F32, name="late", align_bytes=64, offset=0)
         steps = [late[:, l * PACK * V : (l + 1) * PACK * V].rearrange("p (j v) -> p j v", j=PACK) for l in range(3)]
@@ -94,38 +97,34 @@ def tile_picked_tropic_none_p_kernel(
         w2_rows = w2.rearrange("(p j) c -> p j c", j=PACK)
         pairs = [slice(0, 2), slice(2, PACK)]
 
-        def load_step(l, t, rows=slice(0, PACK)):
+        def load_step(l, t, rows):
             nc.sync.dma_start(steps[l][:, rows, :], t.rearrange("(p j) v -> p j v", j=PACK)[:, rows, :])
 
         def load_w2(i):
             nc.sync.dma_start(w2_raw[i], w2_rows[:, :, w2_cuts[i][0] : w2_cuts[i][1]])
 
         load_w2(0)
-        load_step(0, t1, pairs[0])
-        load_step(1, t2, pairs[0])
-        load_step(0, t1, pairs[1])
-        load_step(1, t2, pairs[1])
-        load_step(2, t3)
+        for rows in pairs:
+            for l, t in enumerate((t1, t2, t3)):
+                load_step(l, t, rows)
         load_w2(1)
 
         for h in range(2):
             picked = slice(h * HALF_S, (h + 1) * HALF_S)
             part = offs_t[:, h * HALF_S // LIST_ROWS : (h + 1) * HALF_S // LIST_ROWS]
             nc.vector.tensor_copy(x_codes[:, picked], words[:].bitcast(U32).indirect(part))
-        deal(nc.scalar.copy, 1, 0, 1, 0, P // 2)
-        deal(nc.vector.tensor_copy, 1, 0, 1, P // 2, P)
-        deal(nc.vector.tensor_copy, 1, 1, 2, 0, P)
+        deal(nc.vector.tensor_copy, 0, 0, 2)
+        deal(nc.scalar.copy, 0, 2, PACK)
+        deal(nc.vector.tensor_copy, 1, 0, 1)
+        deal(nc.vector.tensor_copy, 1, 1, 2)
+        deal(nc.scalar.copy, 1, 2, PACK)
         quantize_w1(0, 1, "w1_codes0")
-        deal(nc.scalar.copy, 1, 2, 3, 0, P)
-        deal(nc.scalar.copy, 1, 3, 4, 0, P)
         quantize_w1(1, 2, "w1_codes1")
-        quantize_w1(2, 3, "w1_codes2")
+        quantize_w1(2, PACK, "w1_codes2")
 
         y = [keep.tile([P, S], F32, name=f"y{t}", tag=f"y{t}", align_bytes=64) for t in range(PACK)]
         pieces = [(0, 0, HALF_S), (0, HALF_S, S), (1, 0, S), (2, 0, S), (3, 0, S)]
         for t, s0, s1 in pieces:
-            if (t, s0) == (1, 0):
-                quantize_w1(3, 4, "w1_codes0")
             cols = slice(t * P, (t + 1) * P)
             picked = slice(s0, s1)
             acc = banks.tile([P, s1 - s0], F32, name="acc", tag="bank")
@@ -133,95 +132,93 @@ def tile_picked_tropic_none_p_kernel(
                 acc[:], w1_codes[t].bitcast(FP8X4), w1_planes[:, cols],
                 x_codes[:, picked].bitcast(FP8X4), x_planes[:, picked], start=True, stop=True,
             )
-            engine_copy = nc.vector.tensor_copy if (t, s0) == (0, 0) else nc.scalar.copy
-            engine_copy(y[t][:, picked], acc[:])
+            nc.scalar.copy(y[t][:, picked], acc[:])
 
-        w2_bf = keep.tile([P, N, PACK], BF16, name="w2_bf", align_bytes=64)
+        w2_bf = [keep.tile([P, 2 * P, PACK], BF16, name="w2_bf0", align_bytes=64)]
         w2_planes = keep.tile([P, N], U8, name="w2_planes", align_bytes=64)
-        w2_all = keep.tile([P, N], U32, name="w2_all", tag="codes", align_bytes=64)
+        w2_codes = [keep.tile([P, 2 * P], U32, name="w2_codes0", align_bytes=64)]
 
         def weave_w2(engine_copy, t):
             i, c0 = divmod(t * P, 2 * P)
-            engine_copy(woven(w2_bf[:, t * P : (t + 1) * P, :]), planar(w2_raw[i][:, :, c0 : c0 + P]))
+            engine_copy(woven(w2_bf[i][:, c0 : c0 + P, :]), planar(w2_raw[i][:, :, c0 : c0 + P]))
 
-        def quantize_w2(ta, tb):
-            cols = slice(ta * P, tb * P)
-            nc.vector.quantize_mx(w2_all[:, cols].bitcast(FP8X4), w2_planes[:, cols], w2_bf[:, cols, :].rearrange("p c j -> p (c j)"))
+        def quantize_w2(t):
+            i, c0 = divmod(t * P, 2 * P)
+            nc.vector.quantize_mx(
+                w2_codes[i][:, c0 : c0 + P].bitcast(FP8X4), w2_planes[:, t * P : (t + 1) * P],
+                w2_bf[i][:, c0 : c0 + P, :].rearrange("p c j -> p (c j)"),
+            )
 
-        looked = [keep.tile([P, PACK, V], F32, name=f"looked{l}", align_bytes=64) for l in range(3)]
+        summed = [keep.tile([P, 2, V], F32, name=f"summed{l}", align_bytes=64) for l in range(3)]
+        looked = [
+            keep.tile([P, 2, V], F32, name=f"looked{l}", tag=tag, align_bytes=64)
+            for l, tag in enumerate(("looked0", "codes", "w1_codes2"))
+        ]
         halves = [slice(h * HALF_V, (h + 1) * HALF_V) for h in range(2)]
-        whole = slice(0, V)
-
-        def entries(l, states):
-            return lists[l][:, states.start // LIST_ROWS : states.stop // LIST_ROWS]
 
         def fetch_and_add(l, t):
-            nc.vector.tensor_tensor(looked[l][:, t, :], y[t][:].indirect(lists[l][:]), steps[l][:, t, :], ADD)
+            nc.vector.tensor_tensor(summed[l][:, t, :], y[t][:].indirect(lists[l][:]), steps[l][:, t, :], ADD)
 
-        def fetch(l, t, states):
-            nc.scalar.activation(looked[l][:, t, states], y[t][:].indirect(entries(l, states)), COPY)
+        def fetch(l, t):
+            nc.scalar.activation(looked[l][:, t - 2, :], y[t][:].indirect(lists[l][:]), COPY)
 
-        def add_rounded(dst, l, a, states):
-            nc.vector.tensor_tensor(woven(dst), planar(looked[l][:, pairs[a], states]), planar(steps[l][:, pairs[a], states]), ADD)
+        def add_rounded(dst, l, states):
+            nc.vector.tensor_tensor(woven(dst), planar(looked[l][:, :, states]), planar(steps[l][:, pairs[1], states]), ADD)
 
-        best = keep.tile([P, 2, V, 2], BF16, name="best", align_bytes=64)
-        third = keep.tile([P, 2, V, 2], BF16, name="third", align_bytes=64)
-        second = keep.tile([P, V, 2], BF16, name="second", align_bytes=64)
-        z = [keep.tile([P, HALF_V, PACK], BF16, name=f"z{h}", align_bytes=64) for h in range(2)]
+        z = [keep.tile([P, HALF_V, PACK], BF16, name=f"z{h}", tag=f"z{h}", align_bytes=64) for h in range(2)]
         z_codes = keep.tile([P, V], U32, name="z_codes", align_bytes=64)
         z_planes = keep.tile([P, V], U8, name="z_planes", align_bytes=64)
 
-        def best_of_three(h):
+        for l in range(3):
+            for t in (2, 3):
+                fetch(l, t)
+
+        weave_w2(nc.vector.tensor_copy, 0)
+        weave_w2(nc.vector.tensor_copy, 1)
+        quantize_w2(0)
+        quantize_w2(1)
+        for t in range(2):
+            fetch_and_add(0, t)
+            fetch_and_add(1, t)
+        fetch_and_add(2, 0)
+        fetch_and_add(2, 1)
+
+        sums = keep.tile([P, 2, V, 2], BF16, name="sums", tag="y0", align_bytes=64)
+        add_rounded(sums[:, 0], 0, slice(0, V))
+        add_rounded(sums[:, 1], 1, slice(0, V))
+        best = keep.tile([P, 2, V, 2], BF16, name="best", tag="y1", align_bytes=64)
+        nc.vector.tensor_tensor(woven(best[:, 0]), planar(summed[0][:]), planar(summed[1][:]), MAX)
+        third = keep.tile([P, 2, V, 2], BF16, name="third", tag="y2", align_bytes=64)
+        nc.vector.tensor_tensor(third[:, 1], sums[:, 0], sums[:, 1], MAX)
+        nc.scalar.copy(woven(third[:, 0]), planar(summed[2][:]))
+        w2_bf.append(keep.tile([P, 2 * P, PACK], BF16, name="w2_bf1", tag="y3", align_bytes=64))
+        weave_w2(nc.scalar.copy, 2)
+        weave_w2(nc.scalar.copy, 3)
+        for states in halves:
+            add_rounded(best[:, 1, states, :], 2, states)
+        for h in range(2):
             nc.vector.tensor_tensor(
                 z[h][:].rearrange("p v (a j) -> p v a j", a=2), best[:, :, halves[h], :].rearrange("p a v j -> p v a j"),
                 third[:, :, halves[h], :].rearrange("p a v j -> p v a j"), MAX,
             )
-
-        def quantize_z(h):
+        for h in range(2):
             nc.vector.quantize_mx(z_codes[:, halves[h]].bitcast(FP8X4), z_planes[:, halves[h]], z[h][:].rearrange("p v j -> p (v j)"))
-
-        for t in (2, 3):
-            fetch(1, t, whole)
-        for t in range(PACK):
-            fetch(2, t, whole)
-
-        weave_w2(nc.vector.tensor_copy, 0)
-        weave_w2(nc.vector.tensor_copy, 1)
-        for t in range(2):
-            fetch_and_add(0, t)
-            fetch_and_add(1, t)
-        quantize_w2(0, 2)
-        fetch_and_add(0, 2)
-        fetch_and_add(0, 3)
-        first = keep.tile([P, V, 2], BF16, name="first", tag="y2", align_bytes=64)
-        nc.scalar.copy(woven(first[:]), planar(looked[0][:, pairs[1], :]))
-        weave_w2(nc.scalar.copy, 2)
-        weave_w2(nc.scalar.copy, 3)
-        add_rounded(second[:], 1, 1, whole)
-        nc.vector.tensor_tensor(woven(best[:, 0]), planar(looked[0][:, pairs[0], :]), planar(looked[1][:, pairs[0], :]), MAX)
-        add_rounded(third[:, 0], 2, 0, whole)
-        add_rounded(third[:, 1, halves[0], :], 2, 1, halves[0])
-        nc.vector.tensor_tensor(best[:, 1], first[:], second[:], MAX)
-        add_rounded(third[:, 1, halves[1], :], 2, 1, halves[1])
-        for h in range(2):
-            best_of_three(h)
-        for h in range(2):
-            quantize_z(h)
-        quantize_w2(2, 3)
-        quantize_w2(3, 4)
+        w2_codes.append(keep.tile([P, 2 * P], U32, name="w2_codes1", tag="z0", align_bytes=64))
+        quantize_w2(2)
+        quantize_w2(3)
 
         out_rows = out.rearrange("(a t p) v -> a p t v", a=2, t=2)
 
         def project(t, states, dst, engine_copy):
             acc2 = banks.tile([P, 1, states.stop - states.start], F32, name="acc2", tag="bank")
             nc.tensor.matmul_mx(
-                acc2[:, 0, :], w2_all[:, t * P : (t + 1) * P].bitcast(FP8X4), w2_planes[:, t * P : (t + 1) * P],
+                acc2[:, 0, :], w2_codes[t // 2][:, t % 2 * P : (t % 2 + 1) * P].bitcast(FP8X4), w2_planes[:, t * P : (t + 1) * P],
                 z_codes[:, states].bitcast(FP8X4), z_planes[:, states], start=True, stop=True,
             )
             engine_copy(dst, acc2[:])
 
         low = [keep.tile([P, 2, HALF_V], F32, name=f"low{h}") for h in range(2)]
-        high = [keep.tile([P, 1, V], F32, name=f"high{t}") for t in range(2)]
+        high = [keep.tile([P, 1, V], F32, name=f"high{t}", tag=tag, align_bytes=64) for t, tag in enumerate(("y3", "high1"))]
         for h in range(2):
             for t in range(2):
                 project(t, halves[h], low[h][:, t : t + 1, :], nc.scalar.copy)

@@ -181,15 +181,17 @@ def tile_picked_tropic_none_p_kernel(
             fetch_and_add(0, t)
             fetch_and_add(1, t)
         fetch_and_add(2, 0)
+        best = keep.tile([P, 2, V, 2], BF16, name="best", align_bytes=64)
+        nc.vector.tensor_tensor(woven(best[:, 0]), planar(summed[0][:]), planar(summed[1][:]), MAX)
         fetch_and_add(2, 1)
 
         sums = keep.tile([P, 2, V, 2], BF16, name="sums", tag="y0", align_bytes=64)
         add_rounded(sums[:, 0], 0, slice(0, V))
-        add_rounded(sums[:, 1], 1, slice(0, V))
-        best = keep.tile([P, 2, V, 2], BF16, name="best", tag="y1", align_bytes=64)
-        nc.vector.tensor_tensor(woven(best[:, 0]), planar(summed[0][:]), planar(summed[1][:]), MAX)
+        for states in halves:
+            add_rounded(sums[:, 1, states, :], 1, states)
         third = keep.tile([P, 2, V, 2], BF16, name="third", tag="y2", align_bytes=64)
-        nc.vector.tensor_tensor(third[:, 1], sums[:, 0], sums[:, 1], MAX)
+        for states in halves:
+            nc.vector.tensor_tensor(third[:, 1, states, :], sums[:, 0, states, :], sums[:, 1, states, :], MAX)
         nc.scalar.copy(woven(third[:, 0]), planar(summed[2][:]))
         w2_bf.append(keep.tile([P, 2 * P, PACK], BF16, name="w2_bf1", tag="y3", align_bytes=64))
         weave_w2(nc.scalar.copy, 2)

@@ -41,13 +41,13 @@ def tile_picked_tropic_none_p_kernel(
         reused = ctx.enter_context(tc.tile_pool(name="reused", bufs=1))
         banks = ctx.enter_context(tc.psum_pool(name="banks", bufs=8))
 
-        words = keep.tile([P, T], I32, name="words", align_bytes=64)
-        planes = keep.tile([P, T], U8, name="planes", align_bytes=64)
+        words = keep.tile([P, T], I32, name="words", align_bytes=256)
+        planes = keep.tile([P, T], U8, name="planes", align_bytes=256)
         offs_t = keep.tile([P, S // LIST_ROWS], U16, name="offs_t")
         lists = [keep.tile([P, V // LIST_ROWS], U16, name=f"list{l}") for l in range(3)]
-        w1_raw = [keep.tile([P, 2, H], F32, name=f"w1_raw{a}") for a in range(2)]
-        x_rows = reused.tile([P, S], U8, name="x_rows", align_bytes=64, offset=0)
-        x_planes = keep.tile([P, S], U8, name="x_planes", align_bytes=64)
+        w1_raw = [keep.tile([P, 2, H], F32, name=f"w1_raw{a}", align_bytes=256) for a in range(2)]
+        x_rows = reused.tile([P, S], U8, name="x_rows", align_bytes=256, offset=0)
+        x_planes = keep.tile([P, S], U8, name="x_planes", align_bytes=256)
 
         warm = keep.tile([P, 2], F32, name="warm")
         nc.vector.memset(warm[:, 0:1], 0.0)
@@ -89,7 +89,7 @@ def tile_picked_tropic_none_p_kernel(
                 w1_codes[t] = codes[:, (t - ta) * P : (t - ta + 1) * P]
             nc.vector.quantize_mx(codes[:].bitcast(FP8X4), w1_planes[:, cols], w1_bf[ta // 2][:, ta % 2 : ta % 2 + tb - ta].rearrange("p t m j -> p (t m j)"))
 
-        late = reused.tile([P, 3 * PACK * V + PACK * N], F32, name="late", align_bytes=64, offset=0)
+        late = reused.tile([P, 3 * PACK * V + PACK * N], F32, name="late", align_bytes=256, offset=0)
         steps = [late[:, l * PACK * V : (l + 1) * PACK * V].rearrange("p (j v) -> p j v", j=PACK) for l in range(3)]
         w2_late = late[:, 3 * PACK * V :]
         w2_cuts = [(0, 2 * P), (2 * P, N)]
@@ -122,7 +122,7 @@ def tile_picked_tropic_none_p_kernel(
         quantize_w1(1, 2, "w1_codes1")
         quantize_w1(2, PACK, "w1_codes2")
 
-        y = [keep.tile([P, S], F32, name=f"y{t}", tag=f"y{t}", align_bytes=64) for t in range(PACK)]
+        y = [keep.tile([P, S], F32, name=f"y{t}", tag=f"y{t}", align_bytes=256) for t in range(PACK)]
         pieces = [(0, 0, HALF_S), (0, HALF_S, S), (1, 0, S), (2, 0, S), (3, 0, S)]
         for t, s0, s1 in pieces:
             cols = slice(t * P, (t + 1) * P)
@@ -185,15 +185,15 @@ def tile_picked_tropic_none_p_kernel(
         nc.vector.tensor_tensor(woven(best[:, 0]), planar(summed[0][:]), planar(summed[1][:]), MAX)
         fetch_and_add(2, 1)
 
-        sums = keep.tile([P, 2, V, 2], BF16, name="sums", tag="y0", align_bytes=64)
+        sums = keep.tile([P, 2, V, 2], BF16, name="sums", tag="y0", align_bytes=256)
         add_rounded(sums[:, 0], 0, slice(0, V))
         for states in halves:
             add_rounded(sums[:, 1, states, :], 1, states)
-        third = keep.tile([P, 2, V, 2], BF16, name="third", tag="y2", align_bytes=64)
+        third = keep.tile([P, 2, V, 2], BF16, name="third", tag="y2", align_bytes=256)
         for states in halves:
             nc.vector.tensor_tensor(third[:, 1, states, :], sums[:, 0, states, :], sums[:, 1, states, :], MAX)
         nc.scalar.copy(woven(third[:, 0]), planar(summed[2][:]))
-        w2_bf.append(keep.tile([P, 2 * P, PACK], BF16, name="w2_bf1", tag="y3", align_bytes=64))
+        w2_bf.append(keep.tile([P, 2 * P, PACK], BF16, name="w2_bf1", tag="y3", align_bytes=256))
         weave_w2(nc.scalar.copy, 2)
         weave_w2(nc.scalar.copy, 3)
         for states in halves:
@@ -219,8 +219,8 @@ def tile_picked_tropic_none_p_kernel(
             )
             engine_copy(dst, acc2[:])
 
-        low = [keep.tile([P, 2, HALF_V], F32, name=f"low{h}") for h in range(2)]
-        high = [keep.tile([P, 1, V], F32, name=f"high{t}", tag=tag, align_bytes=64) for t, tag in enumerate(("y3", "high1"))]
+        low = [keep.tile([P, 2, HALF_V], F32, name=f"low{h}", align_bytes=256) for h in range(2)]
+        high = [keep.tile([P, 1, V], F32, name=f"high{t}", tag=tag, align_bytes=256) for t, tag in enumerate(("y3", "high1"))]
         for h in range(2):
             for t in range(2):
                 project(t, halves[h], low[h][:, t : t + 1, :], nc.scalar.copy)

@@ -21,7 +21,7 @@ PACK = 4
 LIST_ROWS = 16
 HALF_S = S // 2
 HALF_V = V // 2
-FIRST_LOAD = 768
+FIRST_LOAD = 640
 
 
 def woven(ap):
@@ -50,15 +50,15 @@ def tile_picked_tropic_none_p_kernel(
         x_planes = keep.tile([P, S], U8, name="x_planes", align_bytes=256)
 
         warm = keep.tile([P, 2], F32, name="warm")
-        nc.vector.memset(warm[:, 0:1], 0.0)
         nc.vector.memset(planes[:].bitcast(I32), 0)
+        nc.vector.memset(warm[:, 0:1], 0.0)
         nc.scalar.copy(warm[:, 1:2], warm[:, 0:1])
         w1_rows = w1.rearrange("(p j) c -> p j c", j=PACK)
         x_rows_hbm = x_words[0].rearrange("p n r -> p (n r)").bitcast(I32)
         nc.sync.dma_start(words[:, :FIRST_LOAD], x_rows_hbm[:, :FIRST_LOAD])
         nc.sync.dma_start(offs_t[:], offs)
-        nc.sync.dma_start(lists[0][:], p1)
         nc.sync.dma_start(planes[0:P:8, :].bitcast(I32), x_scales[0].bitcast(I32))
+        nc.sync.dma_start(lists[0][:], p1)
         nc.sync.dma_start(words[:, FIRST_LOAD:], x_rows_hbm[:, FIRST_LOAD:])
         nc.sync.dma_start(w1_raw[0][:], w1_rows[:, :2, :])
         nc.sync.dma_start(w1_raw[1][:], w1_rows[:, 2:, :])
@@ -123,7 +123,7 @@ def tile_picked_tropic_none_p_kernel(
         quantize_w1(2, PACK, "w1_codes2")
 
         y = [keep.tile([P, S], F32, name=f"y{t}", tag=f"y{t}", align_bytes=256) for t in range(PACK)]
-        pieces = [(0, 0, HALF_S), (0, HALF_S, S), (1, 0, S), (2, 0, S), (3, 0, S)]
+        pieces = [(0, s, s + P) for s in range(0, S, P)] + [(1, 0, HALF_S), (1, HALF_S, S), (2, 0, S), (3, 0, S)]
         for t, s0, s1 in pieces:
             cols = slice(t * P, (t + 1) * P)
             picked = slice(s0, s1)

@@ -123,7 +123,7 @@ def tile_picked_tropic_none_p_kernel(
         quantize_w1(2, PACK, "w1_codes2")
 
         y = [keep.tile([P, S], F32, name=f"y{t}", tag=f"y{t}", align_bytes=256) for t in range(PACK)]
-        pieces = [(0, s, s + P) for s in range(0, S, P)] + [(1, 0, HALF_S), (1, HALF_S, S), (2, 0, S), (3, 0, S)]
+        pieces = [(0, s, s + P) for s in range(0, S, P)] + [(t, s, s + HALF_S) for t in range(1, PACK) for s in (0, HALF_S)]
         for t, s0, s1 in pieces:
             cols = slice(t * P, (t + 1) * P)
             picked = slice(s0, s1)

from contextlib import ExitStack

import concourse.mybir as mybir

K, T, S, V, N, H = 512, 2048, 512, 256, 512, 512
FLOPS = 2 * K * H * S + 2 * H * N * V

F32 = mybir.dt.float32
BF16 = mybir.dt.bfloat16
I32 = mybir.dt.int32
U32 = mybir.dt.uint32
U16 = mybir.dt.uint16
U8 = mybir.dt.uint8
FP8X4 = mybir.dt.float8_e4m3fn_x4
ADD = mybir.AluOpType.add
MAX = mybir.AluOpType.max
COPY = mybir.ActivationFunctionType.Copy

P = 128
PACK = 4
LIST_ROWS = 16
HALF_S = S // 2
HALF_V = V // 2
FIRST_LOAD = 640


def woven(ap):
    return ap.rearrange("p (c i) j -> p c j i", i=4)


def planar(ap):
    return ap.rearrange("p j (c i) -> p c j i", i=4)


def tile_picked_tropic_none_p_kernel(
    tc, x_words, x_scales, w1, t1, t2, t3, w2, offs, p1, p2, p3, out
):
    nc = tc.nc
    with ExitStack() as ctx:
        keep = ctx.enter_context(tc.tile_pool(name="keep", bufs=1))
        reused = ctx.enter_context(tc.tile_pool(name="reused", bufs=1))
        banks = ctx.enter_context(tc.psum_pool(name="banks", bufs=8))

        words = keep.tile([P, T], I32, name="words", align_bytes=256)
        planes = keep.tile([P, T], U8, name="planes", align_bytes=256)
        offs_t = keep.tile([P, S // LIST_ROWS], U16, name="offs_t")
        lists = [keep.tile([P, V // LIST_ROWS], U16, name=f"list{l}") for l in range(3)]
        w1_raw = [keep.tile([P, 2, H], F32, name=f"w1_raw{a}", align_bytes=256) for a in range(2)]
        x_rows = reused.tile([P, S], U8, name="x_rows", align_bytes=256, offset=0)
        x_planes = keep.tile([P, S], U8, name="x_planes", align_bytes=256)

        warm = keep.tile([P, 2], F32, name="warm")
        nc.vector.memset(planes[:].bitcast(I32), 0)
        nc.vector.memset(warm[:, 0:1], 0.0)
        nc.scalar.copy(warm[:, 1:2], warm[:, 0:1])
        w1_rows = w1.rearrange("(p j) c -> p j c", j=PACK)
        x_rows_hbm = x_words[0].rearrange("p n r -> p (n r)").bitcast(I32)
        nc.sync.dma_start(words[:, :FIRST_LOAD], x_rows_hbm[:, :FIRST_LOAD])
        nc.sync.dma_start(offs_t[:], offs)
        nc.sync.dma_start(planes[0:P:8, :].bitcast(I32), x_scales[0].bitcast(I32))
        nc.sync.dma_start(lists[0][:], p1)
        nc.sync.dma_start(words[:, FIRST_LOAD:], x_rows_hbm[:, FIRST_LOAD:])
        nc.sync.dma_start(w1_raw[0][:], w1_rows[:, :2, :])
        nc.sync.dma_start(w1_raw[1][:], w1_rows[:, 2:, :])
        nc.sync.dma_start(lists[1][:], p2)
        nc.sync.dma_start(lists[2][:], p3)
        nc.vector.tensor_copy(x_rows[:], planes[:].indirect(offs_t[:]))
        nc.vector.tensor_copy(x_planes[:].bitcast(I32), x_rows[:].bitcast(I32))
        for r in range(1, 4):
            nc.sync.dma_start(x_planes[r:P:32, :].bitcast(I32), x_planes[8 * r : P : 32, :].bitcast(I32))

        w1_bf = [keep.tile([P, 2, P, PACK], BF16, name=f"w1_bf{b}", align_bytes=64) for b in range(2)]

        def deal(engine_copy, a, t0, t1_):
            b = t0 // 2
            engine_copy(
                w1_bf[b][:, t0 - 2 * b : t1_ - 2 * b, :, 2 * a : 2 * a + 2].rearrange("p t m j -> p m j t"),
                w1_raw[a][:].rearrange("p j (m t) -> p m j t", t=PACK)[:, :, :, t0:t1_],
            )

        x_codes = keep.tile([P, S], U32, name="x_codes", tag="codes", align_bytes=64)
        w1_codes = {}
        w1_planes = keep.tile([P, H], U8, name="w1_planes", align_bytes=64)

        def quantize_w1(ta, tb, tag):
            cols = slice(ta * P, tb * P)
            codes = keep.tile([P, (tb - ta) * P], U32, name=f"w1_codes{ta}", tag=tag, align_bytes=64)
            for t in range(ta, tb):
                w1_codes[t] = codes[:, (t - ta) * P : (t - ta + 1) * P]
            nc.vector.quantize_mx(codes[:].bitcast(FP8X4), w1_planes[:, cols], w1_bf[ta // 2][:, ta % 2 : ta % 2 + tb - ta].rearrange("p t m j -> p (t m j)"))

        late = reused.tile([P, 3 * PACK * V + PACK * N], F32, name="late", align_bytes=256, offset=0)
        steps = [late[:, l * PACK * V : (l + 1) * PACK * V].rearrange("p (j v) -> p j v", j=PACK) for l in range(3)]
        w2_late = late[:, 3 * PACK * V :]
        w2_cuts = [(0, 2 * P), (2 * P, N)]
        w2_raw = [w2_late[:, PACK * c0 : PACK * c1].rearrange("p (j c) -> p j c", j=PACK) for c0, c1 in w2_cuts]
        w2_rows = w2.rearrange("(p j) c -> p j c", j=PACK)
        pairs = [slice(0, 2), slice(2, PACK)]

        def load_step(l, t, rows):
            nc.sync.dma_start(steps[l][:, rows, :], t.rearrange("(p j) v -> p j v", j=PACK)[:, rows, :])

        def load_w2(i):
            nc.sync.dma_start(w2_raw[i], w2_rows[:, :, w2_cuts[i][0] : w2_cuts[i][1]])

        load_w2(0)
        for rows in pairs:
            for l, t in enumerate((t1, t2, t3)):
                load_step(l, t, rows)
        load_w2(1)

        for h in range(2):
            picked = slice(h * HALF_S, (h + 1) * HALF_S)
            part = offs_t[:, h * HALF_S // LIST_ROWS : (h + 1) * HALF_S // LIST_ROWS]
            nc.vector.tensor_copy(x_codes[:, picked], words[:].bitcast(U32).indirect(part))
        deal(nc.vector.tensor_copy, 0, 0, 2)
        deal(nc.scalar.copy, 0, 2, PACK)
        deal(nc.vector.tensor_copy, 1, 0, 1)
        deal(nc.vector.tensor_copy, 1, 1, 2)
        deal(nc.scalar.copy, 1, 2, PACK)
        quantize_w1(0, 1, "w1_codes0")
        quantize_w1(1, 2, "w1_codes1")
        quantize_w1(2, PACK, "w1_codes2")

        y = [keep.tile([P, S], F32, name=f"y{t}", tag=f"y{t}", align_bytes=256) for t in range(PACK)]
        pieces = [(0, s, s + P) for s in range(0, S, P)] + [(t, s, s + HALF_S) for t in range(1, PACK) for s in (0, HALF_S)]
        for t, s0, s1 in pieces:
            cols = slice(t * P, (t + 1) * P)
            picked = slice(s0, s1)
            acc = banks.tile([P, s1 - s0], F32, name="acc", tag="bank")
            nc.tensor.matmul_mx(
                acc[:], w1_codes[t].bitcast(FP8X4), w1_planes[:, cols],
                x_codes[:, picked].bitcast(FP8X4), x_planes[:, picked], start=True, stop=True,
            )
            nc.scalar.copy(y[t][:, picked], acc[:])

        w2_bf = [keep.tile([P, 2 * P, PACK], BF16, name="w2_bf0", align_bytes=64)]
        w2_planes = keep.tile([P, N], U8, name="w2_planes", align_bytes=64)
        w2_codes = [keep.tile([P, 2 * P], U32, name="w2_codes0", align_bytes=64)]

        def weave_w2(engine_copy, t):
            i, c0 = divmod(t * P, 2 * P)
            engine_copy(woven(w2_bf[i][:, c0 : c0 + P, :]), planar(w2_raw[i][:, :, c0 : c0 + P]))

        def quantize_w2(t):
            i, c0 = divmod(t * P, 2 * P)
            nc.vector.quantize_mx(
                w2_codes[i][:, c0 : c0 + P].bitcast(FP8X4), w2_planes[:, t * P : (t + 1) * P],
                w2_bf[i][:, c0 : c0 + P, :].rearrange("p c j -> p (c j)"),
            )

        summed = [keep.tile([P, 2, V], F32, name=f"summed{l}", align_bytes=64) for l in range(3)]
        looked = [
            keep.tile([P, 2, V], F32, name=f"looked{l}", tag=tag, align_bytes=64)
            for l, tag in enumerate(("looked0", "codes", "w1_codes2"))
        ]
        halves = [slice(h * HALF_V, (h + 1) * HALF_V) for h in range(2)]

        def fetch_and_add(l, t):
            nc.vector.tensor_tensor(summed[l][:, t, :], y[t][:].indirect(lists[l][:]), steps[l][:, t, :], ADD)

        def fetch(l, t):
            nc.scalar.activation(looked[l][:, t - 2, :], y[t][:].indirect(lists[l][:]), COPY)

        def add_rounded(dst, l, states):
            nc.vector.tensor_tensor(woven(dst), planar(looked[l][:, :, states]), planar(steps[l][:, pairs[1], states]), ADD)

        z = [keep.tile([P, HALF_V, PACK], BF16, name=f"z{h}", tag=f"z{h}", align_bytes=64) for h in range(2)]
        z_codes = keep.tile([P, V], U32, name="z_codes", align_bytes=64)
        z_planes = keep.tile([P, V], U8, name="z_planes", align_bytes=64)

        for l in range(3):
            for t in (2, 3):
                fetch(l, t)

        weave_w2(nc.vector.tensor_copy, 0)
        weave_w2(nc.vector.tensor_copy, 1)
        quantize_w2(0)
        quantize_w2(1)
        for t in range(2):
            fetch_and_add(0, t)
            fetch_and_add(1, t)
        fetch_and_add(2, 0)
        best = keep.tile([P, 2, V, 2], BF16, name="best", align_bytes=64)
        nc.vector.tensor_tensor(woven(best[:, 0]), planar(summed[0][:]), planar(summed[1][:]), MAX)
        fetch_and_add(2, 1)

        sums = keep.tile([P, 2, V, 2], BF16, name="sums", tag="y0", align_bytes=256)
        add_rounded(sums[:, 0], 0, slice(0, V))
        for states in halves:
            add_rounded(sums[:, 1, states, :], 1, states)
        third = keep.tile([P, 2, V, 2], BF16, name="third", tag="y2", align_bytes=256)
        for states in halves:
            nc.vector.tensor_tensor(third[:, 1, states, :], sums[:, 0, states, :], sums[:, 1, states, :], MAX)
        nc.scalar.copy(woven(third[:, 0]), planar(summed[2][:]))
        w2_bf.append(keep.tile([P, 2 * P, PACK], BF16, name="w2_bf1", tag="y3", align_bytes=256))
        weave_w2(nc.scalar.copy, 2)
        weave_w2(nc.scalar.copy, 3)
        for states in halves:
            add_rounded(best[:, 1, states, :], 2, states)
        for h in range(2):
            nc.vector.tensor_tensor(
                z[h][:].rearrange("p v (a j) -> p v a j", a=2), best[:, :, halves[h], :].rearrange("p a v j -> p v a j"),
                third[:, :, halves[h], :].rearrange("p a v j -> p v a j"), MAX,
            )
        for h in range(2):
            nc.vector.quantize_mx(z_codes[:, halves[h]].bitcast(FP8X4), z_planes[:, halves[h]], z[h][:].rearrange("p v j -> p (v j)"))
        w2_codes.append(keep.tile([P, 2 * P], U32, name="w2_codes1", tag="z0", align_bytes=64))
        quantize_w2(2)
        quantize_w2(3)

        out_rows = out.rearrange("(a t p) v -> a p t v", a=2, t=2)

        def project(t, states, dst, engine_copy):
            acc2 = banks.tile([P, 1, states.stop - states.start], F32, name="acc2", tag="bank")
            nc.tensor.matmul_mx(
                acc2[:, 0, :], w2_codes[t // 2][:, t % 2 * P : (t % 2 + 1) * P].bitcast(FP8X4), w2_planes[:, t * P : (t + 1) * P],
                z_codes[:, states].bitcast(FP8X4), z_planes[:, states], start=True, stop=True,
            )
            engine_copy(dst, acc2[:])

        low = [keep.tile([P, 2, HALF_V], F32, name=f"low{h}", align_bytes=256) for h in range(2)]
        high = [keep.tile([P, 1, V], F32, name=f"high{t}", tag=tag, align_bytes=256) for t, tag in enumerate(("y3", "high1"))]
        for h in range(2):
            for t in range(2):
                project(t, halves[h], low[h][:, t : t + 1, :], nc.scalar.copy)
            nc.sync.dma_start(out_rows[0][:, :, halves[h]], low[h][:])
        for t in range(2):
            for h in range(2):
                project(2 + t, halves[h], high[t][:, :, halves[h]], nc.scalar.copy if h else nc.vector.tensor_copy)
            nc.sync.dma_start(out_rows[1][:, t : t + 1, :], high[t][:])
